import numpy as np
import ml_dtypes


def mxq(x, axis, fmt="e4m3"):
    dtype, down = {"e4m3": (ml_dtypes.float8_e4m3fn, 7), "e5m2": (ml_dtypes.float8_e5m2, 14)}[fmt]
    v = np.moveaxis(np.asarray(x, np.float32).astype(ml_dtypes.bfloat16).astype(np.float64), axis, -1)
    blocks = v.reshape(v.shape[:-1] + (-1, 32))
    amax = np.abs(blocks).max(-1, keepdims=True)
    byte = np.maximum(np.where(amax > 0, np.frexp(amax)[1] - 1 + 127, 0) - down, 1)
    scale = np.exp2(byte - 127.0)
    codes = (blocks / scale).astype(np.float32).astype(dtype).astype(np.float64)
    return np.moveaxis((codes * scale).reshape(v.shape), -1, axis)


WIDE = False


def mx_kscale(k):
    if not WIDE:
        return np.ones(k)
    levels = np.array([10, -10, 5, -5, 0])
    if k % 512:
        return np.exp2(np.random.permutation(np.resize(levels, k // 32))).repeat(32)
    a = np.empty((k // 512, 16))
    for p in range(k // 512):
        a[p, :8] = np.random.permutation(np.resize(levels, 8))
        for g in range(8):
            far = levels[np.abs(levels - a[p, g]) >= 10]
            a[p, g + 8] = far[np.random.randint(len(far))]
    return np.exp2(a.ravel()).repeat(32)


def f64(x):
    return np.asarray(x).astype(np.float64)


def striped(idx):
    return np.tile(idx.reshape(-1, 16).T, (8, 1)).astype(np.uint16)


def unstriped(offs):
    return offs[:16].T.reshape(-1).astype(np.int64)


E2M1 = np.array([0.0, 0.5, 1.0, 1.5, 2.0, 3.0, 4.0, 6.0, -0.0, -0.5, -1.0, -1.5, -2.0, -3.0, -4.0, -6.0])


def pack_weight(w, fmt):
    k, n = w.shape
    w = f64(np.asarray(w, np.float32).astype(ml_dtypes.bfloat16)).reshape(k // 32, 32, n)
    amax = np.abs(w).max(1)
    if fmt == "e4m3":
        byte = np.frexp(amax)[1] - 1 + 127 - 7
    else:
        mant, ex = np.frexp(amax / 6.0)
        byte = np.where(mant > 0.5, ex, ex - 1) + 127
    byte = np.clip(np.where(amax > 0, byte, 1), 1, 254)
    scaled = (w * np.exp2(127.0 - byte)[:, None, :]).reshape(k, n).astype(np.float32)
    by_word = np.ascontiguousarray(scaled.reshape(k // 512, 128, 4, n).transpose(0, 1, 3, 2))
    if fmt == "e4m3":
        words = by_word.astype(ml_dtypes.float8_e4m3fn).view(np.uint8)
    else:
        c = by_word.astype(ml_dtypes.float4_e2m1fn).view(np.uint8) & 0xF
        words = (c[..., 0::2] | (c[..., 1::2] << 4)).reshape(k // 512, 128, 2 * n)
    return np.ascontiguousarray(words), np.ascontiguousarray(byte.astype(np.uint8).reshape(k // 512, 16, n))


def unpack_weight(words, scales, fmt):
    g, _, n = scales.shape
    words = np.ascontiguousarray(words).reshape(g, 128, n, -1)
    if fmt == "e4m3":
        vals = words.view(ml_dtypes.float8_e4m3fn).astype(np.float64)
    else:
        nib = np.empty((g, 128, n, 4), np.uint8)
        nib[..., 0::2] = words & 0xF
        nib[..., 1::2] = words >> 4
        vals = E2M1[nib]
    vals = vals * np.repeat(np.exp2(scales.astype(np.float64) - 127.0), 8, axis=1)[..., None]
    return vals.transpose(0, 1, 3, 2).reshape(g * 512, n)


def gelu(v):
    return 0.5 * v * (1.0 + np.tanh(np.sqrt(2.0 / np.pi) * (v + 0.044715 * v**3)))


K, K2, H, N, T, T2, S = 1024, 512, 1024, 768, 2048, 2048, 1024

def setup_inputs():
    n = np.random.standard_normal
    s, s2, u = mx_kscale(K)[:, None], mx_kscale(K2)[:, None], mx_kscale(H)[:, None]
    tab_words, tab_scales = pack_weight(n((K, T)) * s, "e4m3")
    tab2_words, tab2_scales = pack_weight(n((K2, T2)) * s2, "e4m3")
    wb_words, wb_scales = pack_weight(0.7 * n((K2, H)) / np.sqrt(K2) / s2 * u.T, "e2m1")
    w2_words, w2_scales = pack_weight(n((H, N)) / np.sqrt(H) / u, "e4m3")
    return {
        "tab_words": tab_words, "tab_scales": tab_scales,
        "tab2_words": tab2_words, "tab2_scales": tab2_scales,
        "offs": striped(np.random.permutation(T)[:S]),
        "offs2": striped(np.random.permutation(T2)[:S]),
        "wa": (0.7 * n((K, H)) / np.sqrt(K) / s * u.T).astype(np.float32),
        "wb_words": wb_words, "wb_scales": wb_scales,
        "b": (0.5 * n(H) * u[:, 0]).astype(np.float32),
        "w1": (n((H, N)) / np.sqrt(H) / u).astype(np.float32),
        "w2_words": w2_words, "w2_scales": w2_scales,
        "gT": n((N, T)).astype(np.float32),
    }

def reference(tab_words, tab_scales, tab2_words, tab2_scales, offs, offs2, wa, wb_words, wb_scales, b, w1, w2_words, w2_scales, gT):
    v = unpack_weight(tab_words, tab_scales, "e4m3")[:, unstriped(offs)]
    v2 = unpack_weight(tab2_words, tab2_scales, "e4m3")[:, unstriped(offs2)]
    g = f64(gT)[:, unstriped(offs)]
    wb = unpack_weight(wb_words, wb_scales, "e2m1")
    w2 = unpack_weight(w2_words, w2_scales, "e4m3")
    h = (mxq(f64(wa), 0, "e4m3").T @ v + wb.T @ v2) + f64(b)[:, None]
    hq = mxq(h, 0, "e4m3")
    a = mxq(f64(w1), 0, "e4m3").T @ hq
    q = w2.T @ hq
    return a * (1.0 / (1.0 + np.exp(-q))) + g

@@ -1,0 +1,263 @@
+from contextlib import ExitStack
+
+import concourse.mybir as mybir
+
+K, K2, H, N, T, S = 1024, 512, 1024, 768, 2048, 1024
+FLOPS = 2 * S * (K * H + K2 * H + 2 * H * N)
+
+F32 = mybir.dt.float32
+BF16 = mybir.dt.bfloat16
+I32 = mybir.dt.int32
+U32 = mybir.dt.uint32
+U16 = mybir.dt.uint16
+U8 = mybir.dt.uint8
+FP8X4 = mybir.dt.float8_e4m3fn_x4
+FP4X4 = mybir.dt.float4_e2m1fn_x4
+ACT = mybir.ActivationFunctionType
+ALU = mybir.AluOpType
+
+P = 128
+HALF = 512
+W1_COLS = 256
+LOADS = "wb c a00 t0 a10 g4 t1 a01 g0 a11 g3 g2 v0 g5 g1 w2 v1 v2".split()
+STEPS = "S0 S1 B A00 C1 A11 R11 T0 A01 R10 A10 C0 H00 H10 Q10 W01 T1 H01 W00 W10 H11 Q00 R21 Q11 W21 Q01 O01 W11 O31 O10 O11 R20 O21 R51 R00 W20 R01 O50 O41 O51 F51 R40 O40 F10 O00 R31 R30 F11 O30 F00 R50 F40 O20 R41 F30 F41 F50 F21 F31 F01 F20".split()
+ON_V = "W01 Q10 Q11 A10 A11".split()
+ON_G = "".split()
+ADD_G = "".split()
+SMALL = "cS tS wS".split()
+
+
+def tile_list_routed_code_layer_kernel(
+    tc, tab_words, tab_scales, tab2_words, tab2_scales, offs, offs2, wa, wb_words, wb_scales, b, w1, w2_words, w2_scales, gT, out
+):
+    nc = tc.nc
+    with ExitStack() as ctx:
+        keep = ctx.enter_context(tc.tile_pool(name="keep", bufs=1))
+        ring = ctx.enter_context(tc.tile_pool(name="ring", bufs=2))
+        psum = ctx.enter_context(tc.psum_pool(name="psum", bufs=8))
+
+        def held(shape, dtype, name):
+            return keep.tile(shape, dtype, name=name, align_bytes=64)
+
+        idx = keep.tile([P, S // 16], U16, name="idx")
+        idx2 = keep.tile([P, S // 16], U16, name="idx2")
+        tok_scales = held([P, T // 4], I32, "tok_scales")
+        code_scales = held([P, T // 4], I32, "code_scales")
+        wb_raw = held([P, H // 2], I32, "wb_raw")
+        wb_raw_scales = held([P, H // 4], I32, "wb_raw_scales")
+        wb_codes = held([P, 2 * H], U8, "wb_codes")
+        wb_sc = held([P, H], U8, "wb_sc")
+        bias = held([P, 2, 4], F32, "bias")
+        w2_codes = held([P, 2, N], I32, "w2_codes")
+        w2_sc = held([P, N // 4], I32, "w2_sc")
+        warm = held([P, 8], F32, "warm")
+
+        nc.vector.memset(code_scales[:], 0)
+        nc.gpsimd.memset(tok_scales[:], 0)
+        nc.vector.memset(wb_raw_scales[:], 0)
+        nc.vector.memset(warm[:, 0:4], 0.0)
+        nc.gpsimd.memset(w2_sc[:], 0)
+
+        def words(ap):
+            return ap.rearrange("p t i -> p (t i)").bitcast(I32)
+
+        nc.sync.dma_start(idx2[:], offs2)
+        nc.sync.dma_start(idx[:], offs)
+        for name in SMALL:
+            queue = {"S": nc.scalar, "G": nc.gpsimd, "P": nc.sync}[name[1]]
+            for q in range(4):
+                if name[0] == "c":
+                    queue.dma_start(code_scales[32 * q : 32 * q + 4, :], tab2_scales[0, 4 * q : 4 * q + 4, :].bitcast(I32))
+                elif name[0] == "t":
+                    queue.dma_start(tok_scales[32 * q : 32 * q + 8, :], tab_scales[:, 4 * q : 4 * q + 4, :].bitcast(I32))
+                else:
+                    queue.dma_start(wb_raw_scales[32 * q : 32 * q + 4, :], wb_scales[0, 4 * q : 4 * q + 4, :].bitcast(I32))
+        nc.scalar.activation(warm[:, 4:8], warm[:, 0:4], ACT.Sigmoid)
+        nc.gpsimd.dma_start(bias[:], b.rearrange("(a p t) -> p a t", p=P, t=4))
+        for q in range(4):
+            nc.gpsimd.dma_start(w2_sc[32 * q + 8 : 32 * q + 16, :], w2_scales[:, 4 * q : 4 * q + 4, :].bitcast(I32))
+
+        wa_raw = {}
+        w1_raw = {}
+        windows = {}
+
+        def window(key, dtype, src):
+            windows[key] = ring.tile([P, T], dtype, name="window", bufs=6, align_bytes=64)
+            nc.sync.dma_start(windows[key][:], src)
+
+        def load_wa(g, a):
+            wa_raw[g, a] = ring.tile([P, 4, HALF], F32, name="raw", bufs=4)
+            nc.sync.dma_start(
+                wa_raw[g, a][:], wa[512 * a : 512 * (a + 1), 512 * g : 512 * (g + 1)].rearrange("(p j) c -> p j c", j=4)
+            )
+
+        def load_w1(c):
+            w1_raw[c] = ring.tile([P, 2, 4, W1_COLS], F32, name="raw", bufs=4)
+            for a in range(2):
+                nc.sync.dma_start(
+                    w1_raw[c][:, a],
+                    w1[512 * a : 512 * (a + 1), W1_COLS * c : W1_COLS * (c + 1)].rearrange("(p j) c -> p j c", j=4),
+                )
+
+        for name in LOADS:
+            if name == "c":
+                window("c", I32, words(tab2_words[0]))
+            elif name[0] == "t":
+                window(name, I32, words(tab_words[int(name[1])]))
+            elif name[0] == "g":
+                window(name, F32, gT[P * int(name[1]) : P * (int(name[1]) + 1), :])
+            elif name[0] == "a":
+                load_wa(int(name[1]), int(name[2]))
+            elif name == "wb":
+                nc.sync.dma_start(wb_raw[:], wb_words[0].bitcast(I32))
+            elif name == "w2":
+                nc.sync.dma_start(w2_codes[:], w2_words.rearrange("a p e i -> p a (e i)").bitcast(I32))
+            else:
+                load_w1(int(name[1]))
+        code_words = windows["c"]
+        tok_words = [windows["t0"], windows["t1"]]
+        g_rows = [windows[f"g{n}"] for n in range(6)]
+
+        def offsets(lst, h):
+            return lst[:, 32 * h : 32 * (h + 1)]
+
+        v_words = [[held([P, HALF], U32, f"v_words{a}{h}") for h in range(2)] for a in range(2)]
+        v_sc = [held([P, HALF], U8, f"v_sc{h}") for h in range(2)]
+        c_words = [held([P, HALF], U32, f"c_words{h}") for h in range(2)]
+        c_sc = [held([P, HALF], U8, f"c_sc{h}") for h in range(2)]
+
+        def gather_codes(h):
+            nc.vector.tensor_copy(c_sc[h][:], code_scales[:].bitcast(U8).indirect(offsets(idx2, h)))
+            nc.vector.tensor_copy(c_words[h][:], code_words[:].bitcast(U32).indirect(offsets(idx2, h)))
+
+        def gather_token_scales(h):
+            nc.vector.tensor_copy(v_sc[h][:], tok_scales[:].bitcast(U8).indirect(offsets(idx, h)))
+
+        def gather_tokens(h):
+            for a in range(2):
+                nc.vector.tensor_copy(v_words[a][h][:], tok_words[a][:].bitcast(U32).indirect(offsets(idx, h)))
+
+        def regroup(step, dst, src, four_lines, in_order):
+            if step in ON_G:
+                nc.gpsimd.tensor_scalar(dst, src.rearrange(in_order[0], **in_order[1]), 1.0, 0.0, ALU.mult, ALU.add)
+            else:
+                move = nc.vector.tensor_copy if step in ON_V else nc.scalar.copy
+                move(dst.rearrange(four_lines[0], **four_lines[2]), src.rearrange(four_lines[1], **four_lines[3]))
+
+        def order_wb():
+            nc.vector.tensor_copy(
+                wb_codes[:].bitcast(U16).rearrange("p (g t m) -> p g m t", g=2, t=4),
+                wb_raw[:].bitcast(U16).rearrange("p (g m t) -> p g m t", g=2, t=4),
+            )
+            nc.vector.tensor_copy(
+                wb_sc[:].rearrange("p (g t m) -> p g m t", g=2, t=4),
+                wb_raw_scales[:].bitcast(U8).rearrange("p (g m t) -> p g m t", g=2, t=4),
+            )
+
+        wa_codes = {}
+        wa_sc = {}
+
+        def quantise_wa(g, a):
+            grouped = ring.tile([P, 4 * HALF], BF16, name="grouped", bufs=3, align_bytes=64)
+            regroup(f"A{g}{a}", grouped[:], wa_raw[g, a][:], ("p (t m j) -> p m j t", "p j (m t) -> p m j t", {"t": 4, "j": 4}, {"t": 4}), ("p j (m t) -> p t m j", {"t": 4}))
+            wa_codes[g, a] = held([P, HALF], U32, f"wa_codes{g}{a}")
+            wa_sc[g, a] = held([P, HALF], U8, f"wa_sc{g}{a}")
+            nc.vector.quantize_mx(out=wa_codes[g, a][:].bitcast(FP8X4), scales=wa_sc[g, a][:], in_=grouped[:])
+
+
+        h_codes = {}
+        h_planes = {}
+        h_sc = {}
+
+        def hidden(g, h):
+            planes = ring.tile([P, 4, HALF], BF16, name="h_planes", bufs=3)
+            h_planes[g, h] = planes
+            for t in range(4):
+                acc = psum.tile([P, HALF], F32, name="bank")
+                c0 = HALF * g + P * t
+                nc.tensor.matmul_mx(
+                    out=acc[:],
+                    lhsT=wb_codes[:, 2 * c0 : 2 * (c0 + P)].bitcast(FP4X4),
+                    lhsT_scale=wb_sc[:, c0 : c0 + P],
+                    rhs=c_words[h][:].bitcast(FP8X4),
+                    rhs_scale=c_sc[h][:],
+                    start=True,
+                    stop=False,
+                )
+                for a in range(2):
+                    nc.tensor.matmul_mx(
+                        out=acc[:],
+                        lhsT=wa_codes[g, a][:, P * t : P * (t + 1)].bitcast(FP8X4),
+                        lhsT_scale=wa_sc[g, a][:, P * t : P * (t + 1)],
+                        rhs=v_words[a][h][:].bitcast(FP8X4),
+                        rhs_scale=v_sc[h][4 * a :, :],
+                        start=False,
+                        stop=(a == 1),
+                    )
+                nc.scalar.activation(planes[:, t, :], acc[:], ACT.Identity, bias=bias[:, g, t : t + 1])
+
+        def quantise_h(g, h):
+            planes = h_planes[g, h]
+            grouped = ring.tile([P, 4 * HALF], BF16, name="grouped", bufs=3, align_bytes=64)
+            regroup(f"Q{g}{h}", grouped[:], planes[:], ("p (c i t) -> p c t i", "p t (c i) -> p c t i", {"i": 4, "t": 4}, {"i": 4}), ("p t c -> p c t", {}))
+            h_codes[g, h] = held([P, HALF], U32, f"h_codes{g}{h}")
+            h_sc[g, h] = held([P, HALF], U8, f"h_sc{g}{h}")
+            nc.vector.quantize_mx(out=h_codes[g, h][:].bitcast(FP8X4), scales=h_sc[g, h][:], in_=grouped[:])
+
+        w1_codes = {}
+        w1_sc = {}
+
+        def quantise_w1(c, a):
+            grouped = ring.tile([P, 4 * W1_COLS], BF16, name="grouped", bufs=3, align_bytes=64)
+            regroup(f"W{c}{a}", grouped[:], w1_raw[c][:, a], ("p (c i j) -> p c j i", "p j (c i) -> p c j i", {"i": 4, "j": 4}, {"i": 4}), ("p j c -> p c j", {}))
+            w1_codes[c, a] = held([P, W1_COLS], U32, f"w1_codes{c}{a}")
+            w1_sc[c, a] = held([P, W1_COLS], U8, f"w1_sc{c}{a}")
+            nc.vector.quantize_mx(out=w1_codes[c, a][:].bitcast(FP8X4), scales=w1_sc[c, a][:], in_=grouped[:])
+
+        gated = {}
+        resid = {}
+
+        def output(n, h):
+            c, m0 = divmod(P * n, W1_COLS)
+            gate = psum.tile([P, HALF], F32, name="bank")
+            for g in (1, 0):
+                nc.tensor.matmul_mx(
+                    out=gate[:],
+                    lhsT=w2_codes[:, g, P * n : P * (n + 1)].bitcast(FP8X4),
+                    lhsT_scale=w2_sc[:].bitcast(U8)[8 + 4 * g :, P * n : P * (n + 1)],
+                    rhs=h_codes[g, h][:].bitcast(FP8X4),
+                    rhs_scale=h_sc[g, h][:],
+                    start=(g == 1),
+                    stop=(g == 0),
+                )
+            value = psum.tile([P, HALF], F32, name="bank")
+            for g in (1, 0):
+                nc.tensor.matmul_mx(
+                    out=value[:],
+                    lhsT=w1_codes[c, g][:, m0 : m0 + P].bitcast(FP8X4),
+                    lhsT_scale=w1_sc[c, g][:, m0 : m0 + P],
+                    rhs=h_codes[g, h][:].bitcast(FP8X4),
+                    rhs_scale=h_sc[g, h][:],
+                    start=(g == 1),
+                    stop=(g == 0),
+                )
+            sig = ring.tile([P, HALF], F32, name="sig", bufs=3)
+            nc.scalar.activation(sig[:], gate[:], ACT.Sigmoid)
+            gated[n, h] = ring.tile([P, HALF], F32, name="gated", bufs=12)
+            nc.vector.tensor_tensor(gated[n, h][:], value[:], sig[:], ALU.mult)
+
+        def residual(n, h):
+            resid[n, h] = ring.tile([P, HALF], F32, name="resid", bufs=12)
+            nc.vector.tensor_copy(resid[n, h][:], g_rows[n][:].indirect(offsets(idx, h)))
+
+        def finish(n, h):
+            adder = nc.gpsimd if f"F{n}{h}" in ADD_G else nc.vector
+            adder.tensor_tensor(gated[n, h][:], gated[n, h][:], resid[n, h][:], ALU.add)
+            nc.sync.dma_start(out[P * n : P * (n + 1), HALF * h : HALF * (h + 1)], gated[n, h][:])
+
+        run = {
+            "C": gather_codes, "S": gather_token_scales, "T": gather_tokens, "B": order_wb, "A": quantise_wa, "H": hidden,
+            "Q": quantise_h, "W": quantise_w1, "O": output, "R": residual, "F": finish,
+        }
+        for step in STEPS:
+            run[step[0]](*[int(ch) for ch in step[1:]])

@@ -19,12 +19,13 @@ ALU = mybir.AluOpType
 P = 128
 HALF = 512
 W1_COLS = 256
-LOADS = "wb c a00 t0 a10 g4 t1 a01 g0 a11 g3 g2 v0 g5 g1 w2 v1 v2".split()
-STEPS = "S0 S1 B A00 C1 A11 R11 T0 A01 R10 A10 C0 H00 H10 Q10 W01 T1 H01 W00 W10 H11 Q00 R21 Q11 W21 Q01 O01 W11 O31 O10 O11 R20 O21 R51 R00 W20 R01 O50 O41 O51 F51 R40 O40 F10 O00 R31 R30 F11 O30 F00 R50 F40 O20 R41 F30 F41 F50 F21 F31 F01 F20".split()
-ON_V = "W01 Q10 Q11 A10 A11".split()
+LOADS = "c a11 a10 wb t1 i t0 a00 a01 g3 g1 g5 g0 v2 v0 g2 w2 g4 v1".split()
+STEPS = "R30 C1 C0 W21 A10 A11 R11 R31 B R51 S0 T1 W20 A00 S1 A01 T0 H11 H10 R01 W00 R50 W01 R20 W10 R10 Q11 H01 H00 Q01 Q10 O41 O11 Q00 R41 R40 W11 O01 O50 O10 R00 O40 O31 O00 O30 O51 R21 F31 F50 O21 F00 F51 O20 F30 F40 F11 F41 F21 F01 F10 F20".split()
+ON_V = "Q10 A01 A10 Q01".split()
 ON_G = "".split()
 ADD_G = "".split()
-SMALL = "cS tS wS".split()
+QUEUES = "SPG"
+SMALL = "wG tG cS".split()
 
 
 def tile_list_routed_code_layer_kernel(
@@ -53,16 +54,15 @@ def tile_list_routed_code_layer_kernel(
         warm = held([P, 8], F32, "warm")
 
         nc.vector.memset(code_scales[:], 0)
-        nc.gpsimd.memset(tok_scales[:], 0)
+        nc.vector.memset(tok_scales[:], 0)
         nc.vector.memset(wb_raw_scales[:], 0)
         nc.vector.memset(warm[:, 0:4], 0.0)
-        nc.gpsimd.memset(w2_sc[:], 0)
+        nc.vector.memset(w2_sc[:], 0)
 
         def words(ap):
             return ap.rearrange("p t i -> p (t i)").bitcast(I32)
 
         nc.sync.dma_start(idx2[:], offs2)
-        nc.sync.dma_start(idx[:], offs)
         for name in SMALL:
             queue = {"S": nc.scalar, "G": nc.gpsimd, "P": nc.sync}[name[1]]
             for q in range(4):
@@ -100,7 +100,9 @@ def tile_list_routed_code_layer_kernel(
                 )
 
         for name in LOADS:
-            if name == "c":
+            if name == "i":
+                nc.sync.dma_start(idx[:], offs)
+            elif name == "c":
                 window("c", I32, words(tab2_words[0]))
             elif name[0] == "t":
                 window(name, I32, words(tab_words[int(name[1])]))
@@ -139,27 +141,31 @@ def tile_list_routed_code_layer_kernel(
 
         def regroup(step, dst, src, four_lines, in_order):
             if step in ON_G:
-                nc.gpsimd.tensor_scalar(dst, src.rearrange(in_order[0], **in_order[1]), 1.0, 0.0, ALU.mult, ALU.add)
+                nc.gpsimd.tensor_scalar(dst.rearrange("p (c j) -> p c j", j=4), src.rearrange(in_order[0], **in_order[1]), 1.0, 0.0, ALU.mult, ALU.add)
             else:
                 move = nc.vector.tensor_copy if step in ON_V else nc.scalar.copy
                 move(dst.rearrange(four_lines[0], **four_lines[2]), src.rearrange(four_lines[1], **four_lines[3]))
 
         def order_wb():
             nc.vector.tensor_copy(
-                wb_codes[:].bitcast(U16).rearrange("p (g t m) -> p g m t", g=2, t=4),
-                wb_raw[:].bitcast(U16).rearrange("p (g m t) -> p g m t", g=2, t=4),
+                wb_codes[:].bitcast(U16).rearrange("p (g t m) -> p g t m", g=2, t=4),
+                wb_raw[:].bitcast(U16).rearrange("p (g m t) -> p g t m", g=2, t=4),
             )
             nc.vector.tensor_copy(
-                wb_sc[:].rearrange("p (g t m) -> p g m t", g=2, t=4),
-                wb_raw_scales[:].bitcast(U8).rearrange("p (g m t) -> p g m t", g=2, t=4),
+                wb_sc[:].rearrange("p (g t m) -> p g t m", g=2, t=4),
+                wb_raw_scales[:].bitcast(U8).rearrange("p (g m t) -> p g t m", g=2, t=4),
             )
 
         wa_codes = {}
         wa_sc = {}
 
         def quantise_wa(g, a):
-            grouped = ring.tile([P, 4 * HALF], BF16, name="grouped", bufs=3, align_bytes=64)
-            regroup(f"A{g}{a}", grouped[:], wa_raw[g, a][:], ("p (t m j) -> p m j t", "p j (m t) -> p m j t", {"t": 4, "j": 4}, {"t": 4}), ("p j (m t) -> p t m j", {"t": 4}))
+            grouped = ring.tile([P, 4 * HALF], BF16, name="wa_grouped", bufs=2, align_bytes=64)
+            move = nc.vector.tensor_copy if f"A{g}{a}" in ON_V else nc.scalar.copy
+            dst = grouped[:].rearrange("p (t m j) -> p m j t", t=4, j=4)
+            src = wa_raw[g, a][:].rearrange("p j (m t) -> p m j t", t=4)
+            for t0 in (0, 2):
+                move(dst[:, :, :, t0 : t0 + 2], src[:, :, :, t0 : t0 + 2])
             wa_codes[g, a] = held([P, HALF], U32, f"wa_codes{g}{a}")
             wa_sc[g, a] = held([P, HALF], U8, f"wa_sc{g}{a}")
             nc.vector.quantize_mx(out=wa_codes[g, a][:].bitcast(FP8X4), scales=wa_sc[g, a][:], in_=grouped[:])
@@ -198,7 +204,7 @@ def tile_list_routed_code_layer_kernel(
 
         def quantise_h(g, h):
             planes = h_planes[g, h]
-            grouped = ring.tile([P, 4 * HALF], BF16, name="grouped", bufs=3, align_bytes=64)
+            grouped = ring.tile([P, 4 * HALF], BF16, name="h_grouped", bufs=2, align_bytes=64)
             regroup(f"Q{g}{h}", grouped[:], planes[:], ("p (c i t) -> p c t i", "p t (c i) -> p c t i", {"i": 4, "t": 4}, {"i": 4}), ("p t c -> p c t", {}))
             h_codes[g, h] = held([P, HALF], U32, f"h_codes{g}{h}")
             h_sc[g, h] = held([P, HALF], U8, f"h_sc{g}{h}")
@@ -208,7 +214,7 @@ def tile_list_routed_code_layer_kernel(
         w1_sc = {}
 
         def quantise_w1(c, a):
-            grouped = ring.tile([P, 4 * W1_COLS], BF16, name="grouped", bufs=3, align_bytes=64)
+            grouped = ring.tile([P, 4 * W1_COLS], BF16, name="w1_grouped", bufs=3, align_bytes=64)
             regroup(f"W{c}{a}", grouped[:], w1_raw[c][:, a], ("p (c i j) -> p c j i", "p j (c i) -> p c j i", {"i": 4, "j": 4}, {"i": 4}), ("p j c -> p c j", {}))
             w1_codes[c, a] = held([P, W1_COLS], U32, f"w1_codes{c}{a}")
             w1_sc[c, a] = held([P, W1_COLS], U8, f"w1_sc{c}{a}")
@@ -243,11 +249,11 @@ def tile_list_routed_code_layer_kernel(
                 )
             sig = ring.tile([P, HALF], F32, name="sig", bufs=3)
             nc.scalar.activation(sig[:], gate[:], ACT.Sigmoid)
-            gated[n, h] = ring.tile([P, HALF], F32, name="gated", bufs=12)
+            gated[n, h] = held([P, HALF], F32, f"gated{n}{h}")
             nc.vector.tensor_tensor(gated[n, h][:], value[:], sig[:], ALU.mult)
 
         def residual(n, h):
-            resid[n, h] = ring.tile([P, HALF], F32, name="resid", bufs=12)
+            resid[n, h] = held([P, HALF], F32, f"resid{n}{h}")
             nc.vector.tensor_copy(resid[n, h][:], g_rows[n][:].indirect(offsets(idx, h)))
 
         def finish(n, h):

@@ -19,13 +19,9 @@ ALU = mybir.AluOpType
 P = 128
 HALF = 512
 W1_COLS = 256
-LOADS = "c a11 a10 wb t1 i t0 a00 a01 g3 g1 g5 g0 v2 v0 g2 w2 g4 v1".split()
-STEPS = "R30 C1 C0 W21 A10 A11 R11 R31 B R51 S0 T1 W20 A00 S1 A01 T0 H11 H10 R01 W00 R50 W01 R20 W10 R10 Q11 H01 H00 Q01 Q10 O41 O11 Q00 R41 R40 W11 O01 O50 O10 R00 O40 O31 O00 O30 O51 R21 F31 F50 O21 F00 F51 O20 F30 F40 F11 F41 F21 F01 F10 F20".split()
-ON_V = "Q10 A01 A10 Q01".split()
-ON_G = "".split()
-ADD_G = "".split()
-QUEUES = "SPG"
-SMALL = "wG tG cS".split()
+LOAD_BUFS = 12
+VECTOR_BUFS = 38
+SCALAR_BUFS = 9
 
 
 def tile_list_routed_code_layer_kernel(
@@ -40,230 +36,338 @@ def tile_list_routed_code_layer_kernel(
         def held(shape, dtype, name):
             return keep.tile(shape, dtype, name=name, align_bytes=64)
 
-        idx = keep.tile([P, S // 16], U16, name="idx")
-        idx2 = keep.tile([P, S // 16], U16, name="idx2")
-        tok_scales = held([P, T // 4], I32, "tok_scales")
-        code_scales = held([P, T // 4], I32, "code_scales")
-        wb_raw = held([P, H // 2], I32, "wb_raw")
-        wb_raw_scales = held([P, H // 4], I32, "wb_raw_scales")
-        wb_codes = held([P, 2 * H], U8, "wb_codes")
-        wb_sc = held([P, H], U8, "wb_sc")
-        bias = held([P, 2, 4], F32, "bias")
-        w2_codes = held([P, 2, N], I32, "w2_codes")
-        w2_sc = held([P, N // 4], I32, "w2_sc")
-        warm = held([P, 8], F32, "warm")
+        def loaded(shape, dtype, name, src):
+            tile = ring.tile(shape, dtype, name=name, tag="loaded", bufs=LOAD_BUFS, align_bytes=64)
+            nc.sync.dma_start(tile[:], src)
+            return tile
 
-        nc.vector.memset(code_scales[:], 0)
-        nc.vector.memset(tok_scales[:], 0)
-        nc.vector.memset(wb_raw_scales[:], 0)
-        nc.vector.memset(warm[:, 0:4], 0.0)
-        nc.vector.memset(w2_sc[:], 0)
+        def by_vector(shape, dtype, name):
+            return ring.tile(shape, dtype, name=name, tag="by_vector", bufs=VECTOR_BUFS, align_bytes=64)
+
+        def by_scalar(shape, dtype, name):
+            return ring.tile(shape, dtype, name=name, tag="by_scalar", bufs=SCALAR_BUFS, align_bytes=64)
 
         def words(ap):
             return ap.rearrange("p t i -> p (t i)").bitcast(I32)
 
-        nc.sync.dma_start(idx2[:], offs2)
-        for name in SMALL:
-            queue = {"S": nc.scalar, "G": nc.gpsimd, "P": nc.sync}[name[1]]
+        idx = keep.tile([P, S // 16], U16, name="idx")
+        idx2 = keep.tile([P, S // 16], U16, name="idx2")
+        code_scales = held([P, T // 4], I32, "code_scales")
+        tok_scales = held([P, T // 4], I32, "tok_scales")
+        wb_raw_scales = held([P, H // 4], I32, "wb_raw_scales")
+        w2_sc = held([P, N // 4], I32, "w2_sc")
+        wb_raw = held([P, H // 2], I32, "wb_raw")
+        w2_codes = held([P, 2, N], I32, "w2_codes")
+        bias = held([P, 2, 4], F32, "bias")
+        warm = held([P, 8], F32, "warm")
+
+        nc.vector.memset(code_scales[:], 0)
+        nc.vector.memset(tok_scales[:], 0)
+        nc.vector.memset(warm[:, 0:4], 0.0)
+        nc.vector.memset(wb_raw_scales[:], 0)
+        nc.vector.memset(w2_sc[:], 0)
+
+        def load_one_pass_scales(queue, dst, src):
+            for r in range(4):
+                queue.dma_start(dst[r:P:32, :], src[0, r:16:4, :].bitcast(I32))
+
+        def load_two_pass_scales(queue, dst, src, first):
             for q in range(4):
-                if name[0] == "c":
-                    queue.dma_start(code_scales[32 * q : 32 * q + 4, :], tab2_scales[0, 4 * q : 4 * q + 4, :].bitcast(I32))
-                elif name[0] == "t":
-                    queue.dma_start(tok_scales[32 * q : 32 * q + 8, :], tab_scales[:, 4 * q : 4 * q + 4, :].bitcast(I32))
-                else:
-                    queue.dma_start(wb_raw_scales[32 * q : 32 * q + 4, :], wb_scales[0, 4 * q : 4 * q + 4, :].bitcast(I32))
-        nc.scalar.activation(warm[:, 4:8], warm[:, 0:4], ACT.Sigmoid)
-        nc.gpsimd.dma_start(bias[:], b.rearrange("(a p t) -> p a t", p=P, t=4))
-        for q in range(4):
-            nc.gpsimd.dma_start(w2_sc[32 * q + 8 : 32 * q + 16, :], w2_scales[:, 4 * q : 4 * q + 4, :].bitcast(I32))
-
-        wa_raw = {}
-        w1_raw = {}
-        windows = {}
-
-        def window(key, dtype, src):
-            windows[key] = ring.tile([P, T], dtype, name="window", bufs=6, align_bytes=64)
-            nc.sync.dma_start(windows[key][:], src)
+                queue.dma_start(dst[32 * q + first : 32 * q + first + 8, :], src[:, 4 * q : 4 * q + 4, :].bitcast(I32))
 
         def load_wa(g, a):
-            wa_raw[g, a] = ring.tile([P, 4, HALF], F32, name="raw", bufs=4)
-            nc.sync.dma_start(
-                wa_raw[g, a][:], wa[512 * a : 512 * (a + 1), 512 * g : 512 * (g + 1)].rearrange("(p j) c -> p j c", j=4)
-            )
+            rows = wa[512 * a : 512 * (a + 1), 512 * g : 512 * (g + 1)]
+            return loaded([P, 4, HALF], F32, f"wa_raw{g}{a}", rows.rearrange("(p j) c -> p j c", j=4))
 
         def load_w1(c):
-            w1_raw[c] = ring.tile([P, 2, 4, W1_COLS], F32, name="raw", bufs=4)
+            tile = ring.tile([P, 2, 4, W1_COLS], F32, name=f"w1_raw{c}", tag="loaded", bufs=LOAD_BUFS, align_bytes=64)
             for a in range(2):
-                nc.sync.dma_start(
-                    w1_raw[c][:, a],
-                    w1[512 * a : 512 * (a + 1), W1_COLS * c : W1_COLS * (c + 1)].rearrange("(p j) c -> p j c", j=4),
-                )
+                rows = w1[512 * a : 512 * (a + 1), W1_COLS * c : W1_COLS * (c + 1)]
+                nc.sync.dma_start(tile[:, a], rows.rearrange("(p j) c -> p j c", j=4))
+            return tile
 
-        for name in LOADS:
-            if name == "i":
-                nc.sync.dma_start(idx[:], offs)
-            elif name == "c":
-                window("c", I32, words(tab2_words[0]))
-            elif name[0] == "t":
-                window(name, I32, words(tab_words[int(name[1])]))
-            elif name[0] == "g":
-                window(name, F32, gT[P * int(name[1]) : P * (int(name[1]) + 1), :])
-            elif name[0] == "a":
-                load_wa(int(name[1]), int(name[2]))
-            elif name == "wb":
-                nc.sync.dma_start(wb_raw[:], wb_words[0].bitcast(I32))
-            elif name == "w2":
-                nc.sync.dma_start(w2_codes[:], w2_words.rearrange("a p e i -> p a (e i)").bitcast(I32))
-            else:
-                load_w1(int(name[1]))
-        code_words = windows["c"]
-        tok_words = [windows["t0"], windows["t1"]]
-        g_rows = [windows[f"g{n}"] for n in range(6)]
+        wa_raw = {}
+        tok_words = {}
+
+        nc.sync.dma_start(idx2[:], offs2)
+        load_one_pass_scales(nc.sync, code_scales, tab2_scales)
+        code_words = loaded([P, T], I32, "code_words", words(tab2_words[0]))
+        nc.sync.dma_start(idx[:], offs)
+        wa_raw[0, 0] = load_wa(0, 0)
+        nc.scalar.activation(warm[:, 4:8], warm[:, 0:4], ACT.Sigmoid)
+        load_two_pass_scales(nc.sync, tok_scales, tab_scales, 0)
+        tok_words[0] = loaded([P, T], I32, "tok_words0", words(tab_words[0]))
+        nc.sync.dma_start(wb_raw[:], wb_words[0].bitcast(I32))
+        wa_raw[0, 1] = load_wa(0, 1)
+        load_one_pass_scales(nc.sync, wb_raw_scales, wb_scales)
+        tok_words[1] = loaded([P, T], I32, "tok_words1", words(tab_words[1]))
+        nc.sync.dma_start(bias[:], b.rearrange("(a p t) -> p a t", p=P, t=4))
+        wa_raw[1, 0] = load_wa(1, 0)
+        wa_raw[1, 1] = load_wa(1, 1)
+        load_two_pass_scales(nc.sync, w2_sc, w2_scales, 8)
+        w1_raw = [load_w1(0)]
+        nc.sync.dma_start(w2_codes[:], w2_words.rearrange("a p e i -> p a (e i)").bitcast(I32))
+        g_rows = []
+        for n in range(N // P):
+            g_rows.append(loaded([P, T], F32, f"g_rows{n}", gT[P * n : P * (n + 1), :]))
+            if n in (1, 2):
+                w1_raw.append(load_w1(n))
+
 
         def offsets(lst, h):
             return lst[:, 32 * h : 32 * (h + 1)]
 
-        v_words = [[held([P, HALF], U32, f"v_words{a}{h}") for h in range(2)] for a in range(2)]
-        v_sc = [held([P, HALF], U8, f"v_sc{h}") for h in range(2)]
-        c_words = [held([P, HALF], U32, f"c_words{h}") for h in range(2)]
-        c_sc = [held([P, HALF], U8, f"c_sc{h}") for h in range(2)]
+        def gathered(window, lst, h, dtype, name):
+            dst = by_vector([P, HALF], dtype, name)
+            nc.vector.tensor_copy(dst[:], window[:].bitcast(dtype).indirect(offsets(lst, h)))
+            return dst
+
+        c_sc, c_words, v_sc, v_words = {}, {}, {}, {}
+
+        def gather_code_scales(h):
+            c_sc[h] = gathered(code_scales, idx2, h, U8, f"c_sc{h}")
 
         def gather_codes(h):
-            nc.vector.tensor_copy(c_sc[h][:], code_scales[:].bitcast(U8).indirect(offsets(idx2, h)))
-            nc.vector.tensor_copy(c_words[h][:], code_words[:].bitcast(U32).indirect(offsets(idx2, h)))
+            c_words[h] = gathered(code_words, idx2, h, U32, f"c_words{h}")
 
         def gather_token_scales(h):
-            nc.vector.tensor_copy(v_sc[h][:], tok_scales[:].bitcast(U8).indirect(offsets(idx, h)))
+            v_sc[h] = gathered(tok_scales, idx, h, U8, f"v_sc{h}")
 
-        def gather_tokens(h):
-            for a in range(2):
-                nc.vector.tensor_copy(v_words[a][h][:], tok_words[a][:].bitcast(U32).indirect(offsets(idx, h)))
+        def gather_tokens(a, h):
+            v_words[a, h] = gathered(tok_words[a], idx, h, U32, f"v_words{a}{h}")
 
-        def regroup(step, dst, src, four_lines, in_order):
-            if step in ON_G:
-                nc.gpsimd.tensor_scalar(dst.rearrange("p (c j) -> p c j", j=4), src.rearrange(in_order[0], **in_order[1]), 1.0, 0.0, ALU.mult, ALU.add)
-            else:
-                move = nc.vector.tensor_copy if step in ON_V else nc.scalar.copy
-                move(dst.rearrange(four_lines[0], **four_lines[2]), src.rearrange(four_lines[1], **four_lines[3]))
+        wb = {}
 
         def order_wb():
+            wb["codes"] = by_vector([P, 2 * H], U8, "wb_codes")
             nc.vector.tensor_copy(
-                wb_codes[:].bitcast(U16).rearrange("p (g t m) -> p g t m", g=2, t=4),
+                wb["codes"][:].bitcast(U16).rearrange("p (g t m) -> p g t m", g=2, t=4),
                 wb_raw[:].bitcast(U16).rearrange("p (g m t) -> p g t m", g=2, t=4),
             )
+            wb["scales"] = by_vector([P, H], U8, "wb_sc")
             nc.vector.tensor_copy(
-                wb_sc[:].rearrange("p (g t m) -> p g t m", g=2, t=4),
+                wb["scales"][:].rearrange("p (g t m) -> p g t m", g=2, t=4),
                 wb_raw_scales[:].bitcast(U8).rearrange("p (g m t) -> p g t m", g=2, t=4),
             )
 
-        wa_codes = {}
-        wa_sc = {}
+        def quantised(grouped, name):
+            cols = grouped.shape[1] // 4
+            codes = by_vector([P, cols], U32, name)
+            scales = held([P, cols], U8, name + "_sc")
+            nc.vector.quantize_mx(out=codes[:].bitcast(FP8X4), scales=scales[:], in_=grouped[:])
+            return codes, scales
 
-        def quantise_wa(g, a):
-            grouped = ring.tile([P, 4 * HALF], BF16, name="wa_grouped", bufs=2, align_bytes=64)
-            move = nc.vector.tensor_copy if f"A{g}{a}" in ON_V else nc.scalar.copy
-            dst = grouped[:].rearrange("p (t m j) -> p m j t", t=4, j=4)
-            src = wa_raw[g, a][:].rearrange("p j (m t) -> p m j t", t=4)
-            for t0 in (0, 2):
-                move(dst[:, :, :, t0 : t0 + 2], src[:, :, :, t0 : t0 + 2])
-            wa_codes[g, a] = held([P, HALF], U32, f"wa_codes{g}{a}")
-            wa_sc[g, a] = held([P, HALF], U8, f"wa_sc{g}{a}")
-            nc.vector.quantize_mx(out=wa_codes[g, a][:].bitcast(FP8X4), scales=wa_sc[g, a][:], in_=grouped[:])
+        wa_grouped, wa_q = {}, {}
 
+        def group_wa(g, a, u, on_vector):
+            make, move = (by_vector, nc.vector.tensor_copy) if on_vector else (by_scalar, nc.scalar.copy)
+            grouped = make([P, 2 * HALF], BF16, f"wa_grouped{g}{a}{u}")
+            move(
+                grouped[:].rearrange("p (t m j) -> p m j t", t=2, j=4),
+                wa_raw[g, a][:].rearrange("p j (m t) -> p m j t", t=4)[:, :, :, 2 * u : 2 * u + 2],
+            )
+            wa_grouped[g, a, u] = grouped
 
-        h_codes = {}
-        h_planes = {}
-        h_sc = {}
+        def quantise_wa(g, a, u):
+            wa_q[g, a, u] = quantised(wa_grouped[g, a, u], f"wa_q{g}{a}{u}")
 
-        def hidden(g, h):
-            planes = ring.tile([P, 4, HALF], BF16, name="h_planes", bufs=3)
-            h_planes[g, h] = planes
+        acc = {}
+
+        def code_passes(g, h):
             for t in range(4):
-                acc = psum.tile([P, HALF], F32, name="bank")
                 c0 = HALF * g + P * t
                 nc.tensor.matmul_mx(
-                    out=acc[:],
-                    lhsT=wb_codes[:, 2 * c0 : 2 * (c0 + P)].bitcast(FP4X4),
-                    lhsT_scale=wb_sc[:, c0 : c0 + P],
+                    out=acc[g, h, t][:],
+                    lhsT=wb["codes"][:, 2 * c0 : 2 * (c0 + P)].bitcast(FP4X4),
+                    lhsT_scale=wb["scales"][:, c0 : c0 + P],
                     rhs=c_words[h][:].bitcast(FP8X4),
                     rhs_scale=c_sc[h][:],
-                    start=True,
+                    start=False,
                     stop=False,
                 )
-                for a in range(2):
-                    nc.tensor.matmul_mx(
-                        out=acc[:],
-                        lhsT=wa_codes[g, a][:, P * t : P * (t + 1)].bitcast(FP8X4),
-                        lhsT_scale=wa_sc[g, a][:, P * t : P * (t + 1)],
-                        rhs=v_words[a][h][:].bitcast(FP8X4),
-                        rhs_scale=v_sc[h][4 * a :, :],
-                        start=False,
-                        stop=(a == 1),
-                    )
-                nc.scalar.activation(planes[:, t, :], acc[:], ACT.Identity, bias=bias[:, g, t : t + 1])
+
+        def token_passes(g, h, a):
+            for t in range(4):
+                if a == 0:
+                    acc[g, h, t] = psum.tile([P, HALF], F32, name="bank")
+                codes, scales = wa_q[g, a, t // 2]
+                cols = slice(P * (t % 2), P * (t % 2 + 1))
+                nc.tensor.matmul_mx(
+                    out=acc[g, h, t][:],
+                    lhsT=codes[:, cols].bitcast(FP8X4),
+                    lhsT_scale=scales[:, cols],
+                    rhs=v_words[a, h][:].bitcast(FP8X4),
+                    rhs_scale=v_sc[h][4 * a :, :],
+                    start=(a == 0),
+                    stop=(a == 1),
+                )
+
+        h_planes, h_grouped, h_q = {}, {}, {}
+
+        def empty_hidden(g, h):
+            h_planes[g, h] = by_scalar([P, 4, HALF], BF16, f"h_planes{g}{h}")
+            for t in range(4):
+                nc.scalar.activation(h_planes[g, h][:, t, :], acc[g, h, t][:], ACT.Identity, bias=bias[:, g, t : t + 1])
+
+        def group_h(g, h, u, on_vector):
+            make, move = (by_vector, nc.vector.tensor_copy) if on_vector else (by_scalar, nc.scalar.copy)
+            grouped = make([P, 2 * HALF], BF16, f"h_grouped{g}{h}{u}")
+            move(
+                grouped[:].rearrange("p (c i t) -> p c t i", i=4, t=4),
+                h_planes[g, h][:, :, 256 * u : 256 * (u + 1)].rearrange("p t (c i) -> p c t i", i=4),
+            )
+            h_grouped[g, h, u] = grouped
 
         def quantise_h(g, h):
-            planes = h_planes[g, h]
-            grouped = ring.tile([P, 4 * HALF], BF16, name="h_grouped", bufs=2, align_bytes=64)
-            regroup(f"Q{g}{h}", grouped[:], planes[:], ("p (c i t) -> p c t i", "p t (c i) -> p c t i", {"i": 4, "t": 4}, {"i": 4}), ("p t c -> p c t", {}))
-            h_codes[g, h] = held([P, HALF], U32, f"h_codes{g}{h}")
-            h_sc[g, h] = held([P, HALF], U8, f"h_sc{g}{h}")
-            nc.vector.quantize_mx(out=h_codes[g, h][:].bitcast(FP8X4), scales=h_sc[g, h][:], in_=grouped[:])
+            codes = by_vector([P, HALF], U32, f"h_q{g}{h}")
+            scales = held([P, HALF], U8, f"h_sc{g}{h}")
+            for u in range(2):
+                cols = slice(256 * u, 256 * (u + 1))
+                nc.vector.quantize_mx(out=codes[:, cols].bitcast(FP8X4), scales=scales[:, cols], in_=h_grouped[g, h, u][:])
+            h_q[g, h] = codes, scales
 
-        w1_codes = {}
-        w1_sc = {}
+        w1_grouped, w1_q = {}, {}
+
+        def group_w1(c, a, on_vector):
+            make, move = (by_vector, nc.vector.tensor_copy) if on_vector else (by_scalar, nc.scalar.copy)
+            grouped = make([P, 4 * W1_COLS], BF16, f"w1_grouped{c}{a}")
+            move(
+                grouped[:].rearrange("p (c i j) -> p c j i", i=4, j=4),
+                w1_raw[c][:, a].rearrange("p j (c i) -> p c j i", i=4),
+            )
+            w1_grouped[c, a] = grouped
 
         def quantise_w1(c, a):
-            grouped = ring.tile([P, 4 * W1_COLS], BF16, name="w1_grouped", bufs=3, align_bytes=64)
-            regroup(f"W{c}{a}", grouped[:], w1_raw[c][:, a], ("p (c i j) -> p c j i", "p j (c i) -> p c j i", {"i": 4, "j": 4}, {"i": 4}), ("p j c -> p c j", {}))
-            w1_codes[c, a] = held([P, W1_COLS], U32, f"w1_codes{c}{a}")
-            w1_sc[c, a] = held([P, W1_COLS], U8, f"w1_sc{c}{a}")
-            nc.vector.quantize_mx(out=w1_codes[c, a][:].bitcast(FP8X4), scales=w1_sc[c, a][:], in_=grouped[:])
+            w1_q[c, a] = quantised(w1_grouped[c, a], f"w1_q{c}{a}")
 
-        gated = {}
-        resid = {}
+        value, sig, gated = {}, {}, {}
 
-        def output(n, h):
+        def products(n, h):
             c, m0 = divmod(P * n, W1_COLS)
             gate = psum.tile([P, HALF], F32, name="bank")
-            for g in (1, 0):
+            for g in range(2):
                 nc.tensor.matmul_mx(
                     out=gate[:],
                     lhsT=w2_codes[:, g, P * n : P * (n + 1)].bitcast(FP8X4),
                     lhsT_scale=w2_sc[:].bitcast(U8)[8 + 4 * g :, P * n : P * (n + 1)],
-                    rhs=h_codes[g, h][:].bitcast(FP8X4),
-                    rhs_scale=h_sc[g, h][:],
-                    start=(g == 1),
-                    stop=(g == 0),
+                    rhs=h_q[g, h][0][:].bitcast(FP8X4),
+                    rhs_scale=h_q[g, h][1][:],
+                    start=(g == 0),
+                    stop=(g == 1),
                 )
-            value = psum.tile([P, HALF], F32, name="bank")
-            for g in (1, 0):
+            value[n, h] = psum.tile([P, HALF], F32, name="bank")
+            for g in range(2):
                 nc.tensor.matmul_mx(
-                    out=value[:],
-                    lhsT=w1_codes[c, g][:, m0 : m0 + P].bitcast(FP8X4),
-                    lhsT_scale=w1_sc[c, g][:, m0 : m0 + P],
-                    rhs=h_codes[g, h][:].bitcast(FP8X4),
-                    rhs_scale=h_sc[g, h][:],
-                    start=(g == 1),
-                    stop=(g == 0),
+                    out=value[n, h][:],
+                    lhsT=w1_q[c, g][0][:, m0 : m0 + P].bitcast(FP8X4),
+                    lhsT_scale=w1_q[c, g][1][:, m0 : m0 + P],
+                    rhs=h_q[g, h][0][:].bitcast(FP8X4),
+                    rhs_scale=h_q[g, h][1][:],
+                    start=(g == 0),
+                    stop=(g == 1),
                 )
-            sig = ring.tile([P, HALF], F32, name="sig", bufs=3)
-            nc.scalar.activation(sig[:], gate[:], ACT.Sigmoid)
-            gated[n, h] = held([P, HALF], F32, f"gated{n}{h}")
-            nc.vector.tensor_tensor(gated[n, h][:], value[:], sig[:], ALU.mult)
+            sig[n, h] = by_scalar([P, HALF], F32, f"sig{n}{h}")
+            nc.scalar.activation(sig[n, h][:], gate[:], ACT.Sigmoid)
 
-        def residual(n, h):
-            resid[n, h] = held([P, HALF], F32, f"resid{n}{h}")
-            nc.vector.tensor_copy(resid[n, h][:], g_rows[n][:].indirect(offsets(idx, h)))
+        def gate_value(n, h):
+            gated[n, h] = by_vector([P, HALF], F32, f"gated{n}{h}")
+            nc.vector.tensor_tensor(gated[n, h][:], value[n, h][:], sig[n, h][:], ALU.mult)
 
         def finish(n, h):
-            adder = nc.gpsimd if f"F{n}{h}" in ADD_G else nc.vector
-            adder.tensor_tensor(gated[n, h][:], gated[n, h][:], resid[n, h][:], ALU.add)
-            nc.sync.dma_start(out[P * n : P * (n + 1), HALF * h : HALF * (h + 1)], gated[n, h][:])
+            result = by_vector([P, HALF], F32, f"result{n}{h}")
+            nc.vector.tensor_tensor(result[:], g_rows[n][:].indirect(offsets(idx, h)), gated[n, h][:], ALU.add)
+            nc.sync.dma_start(out[P * n : P * (n + 1), HALF * h : HALF * (h + 1)], result[:])
 
-        run = {
-            "C": gather_codes, "S": gather_token_scales, "T": gather_tokens, "B": order_wb, "A": quantise_wa, "H": hidden,
-            "Q": quantise_h, "W": quantise_w1, "O": output, "R": residual, "F": finish,
-        }
-        for step in STEPS:
-            run[step[0]](*[int(ch) for ch in step[1:]])
+
+        for h in range(2):
+            gather_code_scales(h)
+        for h in range(2):
+            gather_codes(h)
+        group_wa(0, 0, 0, False)
+        group_wa(0, 0, 1, False)
+        for h in range(2):
+            gather_token_scales(h)
+        quantise_wa(0, 0, 0)
+        gather_tokens(0, 0)
+        quantise_wa(0, 0, 1)
+        token_passes(0, 0, 0)
+        gather_tokens(0, 1)
+        token_passes(0, 1, 0)
+        group_wa(0, 1, 0, False)
+        group_wa(0, 1, 1, False)
+        order_wb()
+        code_passes(0, 0)
+        code_passes(0, 1)
+        quantise_wa(0, 1, 0)
+        gather_tokens(1, 0)
+        quantise_wa(0, 1, 1)
+        token_passes(0, 0, 1)
+        gather_tokens(1, 1)
+        token_passes(0, 1, 1)
+        empty_hidden(0, 0)
+        group_wa(1, 0, 0, True)
+        group_wa(1, 0, 1, True)
+        quantise_wa(1, 0, 0)
+        quantise_wa(1, 0, 1)
+        token_passes(1, 0, 0)
+        code_passes(1, 0)
+        empty_hidden(0, 1)
+        group_wa(1, 1, 0, True)
+        group_wa(1, 1, 1, True)
+        quantise_wa(1, 1, 0)
+        quantise_wa(1, 1, 1)
+        token_passes(1, 0, 1)
+        token_passes(1, 1, 0)
+        code_passes(1, 1)
+        token_passes(1, 1, 1)
+        group_h(0, 0, 0, True)
+        group_h(0, 0, 1, True)
+        empty_hidden(1, 0)
+        group_w1(0, 0, True)
+        quantise_h(0, 0)
+        group_w1(0, 1, True)
+        group_h(1, 0, 0, True)
+        group_h(1, 0, 1, True)
+        quantise_w1(0, 0)
+        quantise_h(1, 0)
+        group_h(0, 1, 0, False)
+        empty_hidden(1, 1)
+        quantise_w1(0, 1)
+        products(0, 0)
+        group_h(0, 1, 1, False)
+        products(1, 0)
+        group_h(1, 1, 1, True)
+        gate_value(0, 0)
+        group_h(1, 1, 0, False)
+        finish(0, 0)
+        quantise_h(0, 1)
+        gate_value(1, 0)
+        quantise_h(1, 1)
+        group_w1(1, 0, False)
+        group_w1(1, 1, False)
+        products(0, 1)
+        products(1, 1)
+        finish(1, 0)
+        quantise_w1(1, 0)
+        gate_value(0, 1)
+        quantise_w1(1, 1)
+        products(2, 0)
+        finish(0, 1)
+        gate_value(1, 1)
+        products(2, 1)
+        group_w1(2, 0, False)
+        products(3, 0)
+        group_w1(2, 1, False)
+        finish(1, 1)
+        for n in range(2, 6):
+            gate_value(n, 0)
+            if n < 5:
+                products(n + 1, 1)
+            gate_value(n, 1)
+            finish(n, 0)
+            if n == 2:
+                quantise_w1(2, 0)
+                quantise_w1(2, 1)
+            if n < 4:
+                products(n + 2, 0)
+            finish(n, 1)

@@ -110,8 +110,8 @@ def tile_list_routed_code_layer_kernel(
         g_rows = []
         for n in range(N // P):
             g_rows.append(loaded([P, T], F32, f"g_rows{n}", gT[P * n : P * (n + 1), :]))
-            if n in (1, 2):
-                w1_raw.append(load_w1(n))
+            if n in (2, 3):
+                w1_raw.append(load_w1(n - 1))
 
 
         def offsets(lst, h):
@@ -273,6 +273,16 @@ def tile_list_routed_code_layer_kernel(
             gated[n, h] = by_vector([P, HALF], F32, f"gated{n}{h}")
             nc.vector.tensor_tensor(gated[n, h][:], value[n, h][:], sig[n, h][:], ALU.mult)
 
+        resid = {}
+
+        def residual(n, h):
+            resid[n, h] = by_vector([P, HALF], F32, f"resid{n}{h}")
+            nc.vector.tensor_copy(resid[n, h][:], g_rows[n][:].indirect(offsets(idx, h)))
+
+        def add_residual(n, h, engine):
+            engine.tensor_tensor(gated[n, h][:], gated[n, h][:], resid[n, h][:], ALU.add)
+            nc.sync.dma_start(out[P * n : P * (n + 1), HALF * h : HALF * (h + 1)], gated[n, h][:])
+
         def finish(n, h):
             result = by_vector([P, HALF], F32, f"result{n}{h}")
             nc.vector.tensor_tensor(result[:], g_rows[n][:].indirect(offsets(idx, h)), gated[n, h][:], ALU.add)
@@ -325,49 +335,61 @@ def tile_list_routed_code_layer_kernel(
         empty_hidden(1, 0)
         group_w1(0, 0, True)
         quantise_h(0, 0)
-        group_w1(0, 1, True)
+        group_w1(0, 1, False)
+        quantise_w1(0, 0)
         group_h(1, 0, 0, True)
         group_h(1, 0, 1, True)
-        quantise_w1(0, 0)
-        quantise_h(1, 0)
-        group_h(0, 1, 0, False)
         empty_hidden(1, 1)
+        quantise_h(1, 0)
         quantise_w1(0, 1)
         products(0, 0)
-        group_h(0, 1, 1, False)
+        group_h(0, 1, 0, False)
         products(1, 0)
-        group_h(1, 1, 1, True)
+        group_h(0, 1, 1, False)
+        residual(0, 0)
+        residual(0, 1)
         gate_value(0, 0)
+        add_residual(0, 0, nc.gpsimd)
         group_h(1, 1, 0, False)
-        finish(0, 0)
-        quantise_h(0, 1)
+        group_h(1, 1, 1, False)
+        residual(1, 0)
         gate_value(1, 0)
+        quantise_h(0, 1)
+        add_residual(1, 0, nc.gpsimd)
+        residual(1, 1)
         quantise_h(1, 1)
         group_w1(1, 0, False)
         group_w1(1, 1, False)
         products(0, 1)
         products(1, 1)
-        finish(1, 0)
+        residual(2, 0)
+        residual(2, 1)
         quantise_w1(1, 0)
-        gate_value(0, 1)
         quantise_w1(1, 1)
         products(2, 0)
-        finish(0, 1)
-        gate_value(1, 1)
-        products(2, 1)
         group_w1(2, 0, False)
-        products(3, 0)
+        products(2, 1)
         group_w1(2, 1, False)
-        finish(1, 1)
-        for n in range(2, 6):
-            gate_value(n, 0)
-            if n < 5:
-                products(n + 1, 1)
-            gate_value(n, 1)
-            finish(n, 0)
-            if n == 2:
-                quantise_w1(2, 0)
-                quantise_w1(2, 1)
-            if n < 4:
-                products(n + 2, 0)
-            finish(n, 1)
+        products(3, 0)
+        products(3, 1)
+        gate_value(0, 1)
+        add_residual(0, 1, nc.gpsimd)
+        gate_value(1, 1)
+        add_residual(1, 1, nc.gpsimd)
+        residual(3, 0)
+        gate_value(2, 0)
+        add_residual(2, 0, nc.gpsimd)
+        residual(3, 1)
+        gate_value(2, 1)
+        quantise_w1(2, 0)
+        quantise_w1(2, 1)
+        add_residual(2, 1, nc.gpsimd)
+        for n in (4, 5):
+            products(n, 0)
+            products(n, 1)
+        for n in range(3, 6):
+            for h in range(2):
+                gate_value(n, h)
+                if n > 3:
+                    residual(n, h)
+                add_residual(n, h, nc.vector if (n, h) == (5, 1) else nc.gpsimd)

@@ -20,7 +20,7 @@ P = 128
 HALF = 512
 W1_COLS = 256
 LOAD_BUFS = 12
-VECTOR_BUFS = 38
+VECTOR_BUFS = 37
 SCALAR_BUFS = 9
 
 
@@ -102,17 +102,25 @@ def tile_list_routed_code_layer_kernel(
         load_one_pass_scales(nc.sync, wb_raw_scales, wb_scales)
         tok_words[1] = loaded([P, T], I32, "tok_words1", words(tab_words[1]))
         nc.sync.dma_start(bias[:], b.rearrange("(a p t) -> p a t", p=P, t=4))
+        g_rows = []
+        w1_raw = []
+
+        def load_g(n):
+            g_rows.append(loaded([P, T], F32, f"g_rows{n}", gT[P * n : P * (n + 1), :]))
+
         wa_raw[1, 0] = load_wa(1, 0)
         wa_raw[1, 1] = load_wa(1, 1)
         load_two_pass_scales(nc.sync, w2_sc, w2_scales, 8)
-        w1_raw = [load_w1(0)]
+        w1_raw.append(load_w1(0))
         nc.sync.dma_start(w2_codes[:], w2_words.rearrange("a p e i -> p a (e i)").bitcast(I32))
-        g_rows = []
-        for n in range(N // P):
-            g_rows.append(loaded([P, T], F32, f"g_rows{n}", gT[P * n : P * (n + 1), :]))
-            if n in (2, 3):
-                w1_raw.append(load_w1(n - 1))
-
+        load_g(0)
+        load_g(1)
+        w1_raw.append(load_w1(1))
+        load_g(2)
+        w1_raw.append(load_w1(2))
+        load_g(3)
+        load_g(4)
+        load_g(5)
 
         def offsets(lst, h):
             return lst[:, 32 * h : 32 * (h + 1)]
@@ -172,8 +180,17 @@ def tile_list_routed_code_layer_kernel(
             wa_q[g, a, u] = quantised(wa_grouped[g, a, u], f"wa_q{g}{a}{u}")
 
         acc = {}
+        runs = {}
+
+        def next_run(g, h):
+            runs[g, h] = runs.get((g, h), -1) + 1
+            if runs[g, h] == 0:
+                for t in range(4):
+                    acc[g, h, t] = psum.tile([P, HALF], F32, name="bank")
+            return runs[g, h] == 0, runs[g, h] == 2
 
         def code_passes(g, h):
+            first, last = next_run(g, h)
             for t in range(4):
                 c0 = HALF * g + P * t
                 nc.tensor.matmul_mx(
@@ -182,14 +199,13 @@ def tile_list_routed_code_layer_kernel(
                     lhsT_scale=wb["scales"][:, c0 : c0 + P],
                     rhs=c_words[h][:].bitcast(FP8X4),
                     rhs_scale=c_sc[h][:],
-                    start=False,
-                    stop=False,
+                    start=first,
+                    stop=last,
                 )
 
         def token_passes(g, h, a):
+            first, last = next_run(g, h)
             for t in range(4):
-                if a == 0:
-                    acc[g, h, t] = psum.tile([P, HALF], F32, name="bank")
                 codes, scales = wa_q[g, a, t // 2]
                 cols = slice(P * (t % 2), P * (t % 2 + 1))
                 nc.tensor.matmul_mx(
@@ -198,8 +214,8 @@ def tile_list_routed_code_layer_kernel(
                     lhsT_scale=scales[:, cols],
                     rhs=v_words[a, h][:].bitcast(FP8X4),
                     rhs_scale=v_sc[h][4 * a :, :],
-                    start=(a == 0),
-                    stop=(a == 1),
+                    start=first,
+                    stop=last,
                 )
 
         h_planes, h_grouped, h_q = {}, {}, {}
@@ -209,8 +225,13 @@ def tile_list_routed_code_layer_kernel(
             for t in range(4):
                 nc.scalar.activation(h_planes[g, h][:, t, :], acc[g, h, t][:], ACT.Identity, bias=bias[:, g, t : t + 1])
 
+        def handed_on(shape, dtype, name):
+            return ring.tile(shape, dtype, name=name, tag="handed_on", bufs=2, align_bytes=64)
+
         def group_h(g, h, u, on_vector):
             make, move = (by_vector, nc.vector.tensor_copy) if on_vector else (by_scalar, nc.scalar.copy)
+            if (g, h) == (1, 0):
+                make = handed_on
             grouped = make([P, 2 * HALF], BF16, f"h_grouped{g}{h}{u}")
             move(
                 grouped[:].rearrange("p (c i t) -> p c t i", i=4, t=4),
@@ -218,10 +239,22 @@ def tile_list_routed_code_layer_kernel(
             )
             h_grouped[g, h, u] = grouped
 
+        def group_h_on_gpsimd(g, h, u):
+            grouped = handed_on([P, 2 * HALF], BF16, f"h_grouped{g}{h}{u}")
+            nc.gpsimd.tensor_scalar(
+                grouped[:].rearrange("p (c t) -> p c t", t=4),
+                h_planes[g, h][:, :, 256 * u : 256 * (u + 1)].rearrange("p t c -> p c t"),
+                1.0,
+                0.0,
+                ALU.mult,
+                ALU.add,
+            )
+            h_grouped[g, h, u] = grouped
+
         def quantise_h(g, h):
             codes = by_vector([P, HALF], U32, f"h_q{g}{h}")
             scales = held([P, HALF], U8, f"h_sc{g}{h}")
-            for u in range(2):
+            for u in (1, 0):
                 cols = slice(256 * u, 256 * (u + 1))
                 nc.vector.quantize_mx(out=codes[:, cols].bitcast(FP8X4), scales=scales[:, cols], in_=h_grouped[g, h, u][:])
             h_q[g, h] = codes, scales
@@ -230,10 +263,11 @@ def tile_list_routed_code_layer_kernel(
 
         def group_w1(c, a, on_vector):
             make, move = (by_vector, nc.vector.tensor_copy) if on_vector else (by_scalar, nc.scalar.copy)
+            src = w1_raw[c][:, a]
             grouped = make([P, 4 * W1_COLS], BF16, f"w1_grouped{c}{a}")
             move(
                 grouped[:].rearrange("p (c i j) -> p c j i", i=4, j=4),
-                w1_raw[c][:, a].rearrange("p j (c i) -> p c j i", i=4),
+                src.rearrange("p j (c i) -> p c j i", i=4),
             )
             w1_grouped[c, a] = grouped
 
@@ -283,10 +317,14 @@ def tile_list_routed_code_layer_kernel(
             engine.tensor_tensor(gated[n, h][:], gated[n, h][:], resid[n, h][:], ALU.add)
             nc.sync.dma_start(out[P * n : P * (n + 1), HALF * h : HALF * (h + 1)], gated[n, h][:])
 
-        def finish(n, h):
-            result = by_vector([P, HALF], F32, f"result{n}{h}")
-            nc.vector.tensor_tensor(result[:], g_rows[n][:].indirect(offsets(idx, h)), gated[n, h][:], ALU.add)
-            nc.sync.dma_start(out[P * n : P * (n + 1), HALF * h : HALF * (h + 1)], result[:])
+        def finish(n, h, pieces=1):
+            width = HALF // pieces
+            for c0 in range(0, HALF, width):
+                j0 = HALF * h + c0
+                result = by_vector([P, width], F32, f"result{n}{h}{c0}")
+                picks = idx[:, j0 // 16 : (j0 + width) // 16]
+                nc.vector.tensor_tensor(result[:], g_rows[n][:].indirect(picks), gated[n, h][:, c0 : c0 + width], ALU.add)
+                nc.sync.dma_start(out[P * n : P * (n + 1), j0 : j0 + width], result[:])
 
 
         for h in range(2):
@@ -319,17 +357,17 @@ def tile_list_routed_code_layer_kernel(
         group_wa(1, 0, 1, True)
         quantise_wa(1, 0, 0)
         quantise_wa(1, 0, 1)
-        token_passes(1, 0, 0)
         code_passes(1, 0)
+        token_passes(1, 0, 0)
         empty_hidden(0, 1)
         group_wa(1, 1, 0, True)
         group_wa(1, 1, 1, True)
         quantise_wa(1, 1, 0)
         quantise_wa(1, 1, 1)
         token_passes(1, 0, 1)
-        token_passes(1, 1, 0)
-        code_passes(1, 1)
         token_passes(1, 1, 1)
+        code_passes(1, 1)
+        token_passes(1, 1, 0)
         group_h(0, 0, 0, True)
         group_h(0, 0, 1, True)
         empty_hidden(1, 0)
@@ -340,56 +378,59 @@ def tile_list_routed_code_layer_kernel(
         group_h(1, 0, 0, True)
         group_h(1, 0, 1, True)
         empty_hidden(1, 1)
-        quantise_h(1, 0)
         quantise_w1(0, 1)
+        quantise_h(1, 0)
+        group_h_on_gpsimd(0, 1, 0)
+        group_h_on_gpsimd(0, 1, 1)
         products(0, 0)
-        group_h(0, 1, 0, False)
+        group_h(1, 1, 0, False)
         products(1, 0)
-        group_h(0, 1, 1, False)
+        group_h(1, 1, 1, False)
         residual(0, 0)
         residual(0, 1)
         gate_value(0, 0)
         add_residual(0, 0, nc.gpsimd)
-        group_h(1, 1, 0, False)
-        group_h(1, 1, 1, False)
         residual(1, 0)
         gate_value(1, 0)
         quantise_h(0, 1)
-        add_residual(1, 0, nc.gpsimd)
-        residual(1, 1)
         quantise_h(1, 1)
+        add_residual(1, 0, nc.gpsimd)
         group_w1(1, 0, False)
-        group_w1(1, 1, False)
         products(0, 1)
+        group_w1(1, 1, False)
         products(1, 1)
+        residual(1, 1)
         residual(2, 0)
-        residual(2, 1)
+        gate_value(0, 1)
         quantise_w1(1, 0)
         quantise_w1(1, 1)
+        add_residual(0, 1, nc.gpsimd)
         products(2, 0)
         group_w1(2, 0, False)
         products(2, 1)
         group_w1(2, 1, False)
         products(3, 0)
         products(3, 1)
-        gate_value(0, 1)
-        add_residual(0, 1, nc.gpsimd)
         gate_value(1, 1)
         add_residual(1, 1, nc.gpsimd)
+        residual(2, 1)
         residual(3, 0)
         gate_value(2, 0)
-        add_residual(2, 0, nc.gpsimd)
-        residual(3, 1)
-        gate_value(2, 1)
         quantise_w1(2, 0)
         quantise_w1(2, 1)
-        add_residual(2, 1, nc.gpsimd)
+        add_residual(2, 0, nc.gpsimd)
         for n in (4, 5):
             products(n, 0)
             products(n, 1)
-        for n in range(3, 6):
+        gate_value(2, 1)
+        add_residual(2, 1, nc.gpsimd)
+        residual(3, 1)
+        for h in range(2):
+            gate_value(3, h)
+            add_residual(3, h, nc.gpsimd)
+        for n in (4, 5):
             for h in range(2):
                 gate_value(n, h)
-                if n > 3:
-                    residual(n, h)
-                add_residual(n, h, nc.vector if (n, h) == (5, 1) else nc.gpsimd)
+        for n in (4, 5):
+            for h in range(2):
+                finish(n, h, 2 if (n, h) == (5, 1) else 1)

@@ -17,8 +17,11 @@ ACT = mybir.ActivationFunctionType
 ALU = mybir.AluOpType
 
 P = 128
+PASS = 512
 HALF = 512
+QUARTER = HALF // 2
 W1_COLS = 256
+W2_SCALE_ROW = 8
 LOAD_BUFS = 12
 VECTOR_BUFS = 37
 SCALAR_BUFS = 9
@@ -36,10 +39,8 @@ def tile_list_routed_code_layer_kernel(
         def held(shape, dtype, name):
             return keep.tile(shape, dtype, name=name, align_bytes=64)
 
-        def loaded(shape, dtype, name, src):
-            tile = ring.tile(shape, dtype, name=name, tag="loaded", bufs=LOAD_BUFS, align_bytes=64)
-            nc.sync.dma_start(tile[:], src)
-            return tile
+        def for_load(shape, dtype, name):
+            return ring.tile(shape, dtype, name=name, tag="loaded", bufs=LOAD_BUFS, align_bytes=64)
 
         def by_vector(shape, dtype, name):
             return ring.tile(shape, dtype, name=name, tag="by_vector", bufs=VECTOR_BUFS, align_bytes=64)
@@ -47,8 +48,12 @@ def tile_list_routed_code_layer_kernel(
         def by_scalar(shape, dtype, name):
             return ring.tile(shape, dtype, name=name, tag="by_scalar", bufs=SCALAR_BUFS, align_bytes=64)
 
-        def words(ap):
-            return ap.rearrange("p t i -> p (t i)").bitcast(I32)
+        def handed_on(shape, dtype, name):
+            return ring.tile(shape, dtype, name=name, tag="handed_on", bufs=2, align_bytes=64)
+
+        on_vector = (by_vector, nc.vector.tensor_copy)
+        on_vector_handed_on = (handed_on, nc.vector.tensor_copy)
+        on_scalar = (by_scalar, nc.scalar.copy)
 
         idx = keep.tile([P, S // 16], U16, name="idx")
         idx2 = keep.tile([P, S // 16], U16, name="idx2")
@@ -67,67 +72,68 @@ def tile_list_routed_code_layer_kernel(
         nc.vector.memset(wb_raw_scales[:], 0)
         nc.vector.memset(w2_sc[:], 0)
 
-        def load_one_pass_scales(queue, dst, src):
-            for r in range(4):
-                queue.dma_start(dst[r:P:32, :], src[0, r:16:4, :].bitcast(I32))
-
-        def load_two_pass_scales(queue, dst, src, first):
-            for q in range(4):
-                queue.dma_start(dst[32 * q + first : 32 * q + first + 8, :], src[:, 4 * q : 4 * q + 4, :].bitcast(I32))
-
-        def load_wa(g, a):
-            rows = wa[512 * a : 512 * (a + 1), 512 * g : 512 * (g + 1)]
-            return loaded([P, 4, HALF], F32, f"wa_raw{g}{a}", rows.rearrange("(p j) c -> p j c", j=4))
-
-        def load_w1(c):
-            tile = ring.tile([P, 2, 4, W1_COLS], F32, name=f"w1_raw{c}", tag="loaded", bufs=LOAD_BUFS, align_bytes=64)
-            for a in range(2):
-                rows = w1[512 * a : 512 * (a + 1), W1_COLS * c : W1_COLS * (c + 1)]
-                nc.sync.dma_start(tile[:, a], rows.rearrange("(p j) c -> p j c", j=4))
+        def load(shape, dtype, name, src):
+            tile = for_load(shape, dtype, name)
+            nc.sync.dma_start(tile[:], src)
             return tile
 
-        wa_raw = {}
-        tok_words = {}
+        def load_words(table_pass, name):
+            return load([P, T], I32, name, table_pass.rearrange("p t i -> p (t i)").bitcast(I32))
 
+        def load_one_pass_scales(dst, src):
+            for r in range(4):
+                nc.sync.dma_start(dst[r:P:32, :], src[0, r:16:4, :].bitcast(I32))
+
+        def load_two_pass_scales(dst, src, first_row):
+            for quad in range(4):
+                p0 = 32 * quad + first_row
+                nc.sync.dma_start(dst[p0 : p0 + 8, :], src[:, 4 * quad : 4 * quad + 4, :].bitcast(I32))
+
+        def load_wa(g, a):
+            rows = wa[PASS * a : PASS * (a + 1), PASS * g : PASS * (g + 1)]
+            return load([P, 4, PASS], F32, f"wa_raw{g}{a}", rows.rearrange("(p j) m -> p j m", j=4))
+
+        def load_w1(c):
+            tile = for_load([P, 2, 4, W1_COLS], F32, f"w1_raw{c}")
+            for g in range(2):
+                rows = w1[PASS * g : PASS * (g + 1), W1_COLS * c : W1_COLS * (c + 1)]
+                nc.sync.dma_start(tile[:, g], rows.rearrange("(p j) m -> p j m", j=4))
+            return tile
+
+        def load_g_rows(n):
+            return load([P, T], F32, f"g_rows{n}", gT[P * n : P * (n + 1), :])
+
+        wa_raw, tok_words, w1_raw, g_rows = {}, {}, {}, {}
         nc.sync.dma_start(idx2[:], offs2)
-        load_one_pass_scales(nc.sync, code_scales, tab2_scales)
-        code_words = loaded([P, T], I32, "code_words", words(tab2_words[0]))
+        load_one_pass_scales(code_scales, tab2_scales)
+        code_words = load_words(tab2_words[0], "code_words")
         nc.sync.dma_start(idx[:], offs)
         wa_raw[0, 0] = load_wa(0, 0)
         nc.scalar.activation(warm[:, 4:8], warm[:, 0:4], ACT.Sigmoid)
-        load_two_pass_scales(nc.sync, tok_scales, tab_scales, 0)
-        tok_words[0] = loaded([P, T], I32, "tok_words0", words(tab_words[0]))
+        load_two_pass_scales(tok_scales, tab_scales, 0)
+        tok_words[0] = load_words(tab_words[0], "tok_words0")
         nc.sync.dma_start(wb_raw[:], wb_words[0].bitcast(I32))
         wa_raw[0, 1] = load_wa(0, 1)
-        load_one_pass_scales(nc.sync, wb_raw_scales, wb_scales)
-        tok_words[1] = loaded([P, T], I32, "tok_words1", words(tab_words[1]))
-        nc.sync.dma_start(bias[:], b.rearrange("(a p t) -> p a t", p=P, t=4))
-        g_rows = []
-        w1_raw = []
-
-        def load_g(n):
-            g_rows.append(loaded([P, T], F32, f"g_rows{n}", gT[P * n : P * (n + 1), :]))
-
+        load_one_pass_scales(wb_raw_scales, wb_scales)
+        tok_words[1] = load_words(tab_words[1], "tok_words1")
+        nc.sync.dma_start(bias[:], b.rearrange("(g p t) -> p g t", p=P, t=4))
         wa_raw[1, 0] = load_wa(1, 0)
         wa_raw[1, 1] = load_wa(1, 1)
-        load_two_pass_scales(nc.sync, w2_sc, w2_scales, 8)
-        w1_raw.append(load_w1(0))
-        nc.sync.dma_start(w2_codes[:], w2_words.rearrange("a p e i -> p a (e i)").bitcast(I32))
-        load_g(0)
-        load_g(1)
-        w1_raw.append(load_w1(1))
-        load_g(2)
-        w1_raw.append(load_w1(2))
-        load_g(3)
-        load_g(4)
-        load_g(5)
+        w1_raw[0] = load_w1(0)
+        load_two_pass_scales(w2_sc, w2_scales, W2_SCALE_ROW)
+        nc.sync.dma_start(w2_codes[:], w2_words.rearrange("g p e i -> p g (e i)").bitcast(I32))
+        g_rows[0] = load_g_rows(0)
+        for n in range(1, N // P):
+            g_rows[n] = load_g_rows(n)
+            if n < N // W1_COLS:
+                w1_raw[n] = load_w1(n)
 
-        def offsets(lst, h):
-            return lst[:, 32 * h : 32 * (h + 1)]
+        def offsets(lst, first, count):
+            return lst[:, first // 16 : (first + count) // 16]
 
         def gathered(window, lst, h, dtype, name):
             dst = by_vector([P, HALF], dtype, name)
-            nc.vector.tensor_copy(dst[:], window[:].bitcast(dtype).indirect(offsets(lst, h)))
+            nc.vector.tensor_copy(dst[:], window[:].bitcast(dtype).indirect(offsets(lst, HALF * h, HALF)))
             return dst
 
         c_sc, c_words, v_sc, v_words = {}, {}, {}, {}
@@ -167,9 +173,9 @@ def tile_list_routed_code_layer_kernel(
 
         wa_grouped, wa_q = {}, {}
 
-        def group_wa(g, a, u, on_vector):
-            make, move = (by_vector, nc.vector.tensor_copy) if on_vector else (by_scalar, nc.scalar.copy)
-            grouped = make([P, 2 * HALF], BF16, f"wa_grouped{g}{a}{u}")
+        def group_wa(g, a, u, who):
+            make, move = who
+            grouped = make([P, 2 * PASS], BF16, f"wa_grouped{g}{a}{u}")
             move(
                 grouped[:].rearrange("p (t m j) -> p m j t", t=2, j=4),
                 wa_raw[g, a][:].rearrange("p j (m t) -> p m j t", t=4)[:, :, :, 2 * u : 2 * u + 2],
@@ -179,24 +185,24 @@ def tile_list_routed_code_layer_kernel(
         def quantise_wa(g, a, u):
             wa_q[g, a, u] = quantised(wa_grouped[g, a, u], f"wa_q{g}{a}{u}")
 
-        acc = {}
-        runs = {}
+        acc, runs_done = {}, {}
 
         def next_run(g, h):
-            runs[g, h] = runs.get((g, h), -1) + 1
-            if runs[g, h] == 0:
+            run = runs_done.get((g, h), 0)
+            runs_done[g, h] = run + 1
+            if run == 0:
                 for t in range(4):
                     acc[g, h, t] = psum.tile([P, HALF], F32, name="bank")
-            return runs[g, h] == 0, runs[g, h] == 2
+            return run == 0, run == 2
 
         def code_passes(g, h):
             first, last = next_run(g, h)
             for t in range(4):
-                c0 = HALF * g + P * t
+                col = PASS * g + P * t
                 nc.tensor.matmul_mx(
                     out=acc[g, h, t][:],
-                    lhsT=wb["codes"][:, 2 * c0 : 2 * (c0 + P)].bitcast(FP4X4),
-                    lhsT_scale=wb["scales"][:, c0 : c0 + P],
+                    lhsT=wb["codes"][:, 2 * col : 2 * (col + P)].bitcast(FP4X4),
+                    lhsT_scale=wb["scales"][:, col : col + P],
                     rhs=c_words[h][:].bitcast(FP8X4),
                     rhs_scale=c_sc[h][:],
                     start=first,
@@ -218,32 +224,27 @@ def tile_list_routed_code_layer_kernel(
                     stop=last,
                 )
 
-        h_planes, h_grouped, h_q = {}, {}, {}
+        h_rows, h_grouped, h_q = {}, {}, {}
 
         def empty_hidden(g, h):
-            h_planes[g, h] = by_scalar([P, 4, HALF], BF16, f"h_planes{g}{h}")
+            h_rows[g, h] = by_scalar([P, 4, HALF], BF16, f"h_rows{g}{h}")
             for t in range(4):
-                nc.scalar.activation(h_planes[g, h][:, t, :], acc[g, h, t][:], ACT.Identity, bias=bias[:, g, t : t + 1])
+                nc.scalar.activation(h_rows[g, h][:, t, :], acc[g, h, t][:], ACT.Identity, bias=bias[:, g, t : t + 1])
 
-        def handed_on(shape, dtype, name):
-            return ring.tile(shape, dtype, name=name, tag="handed_on", bufs=2, align_bytes=64)
-
-        def group_h(g, h, u, on_vector):
-            make, move = (by_vector, nc.vector.tensor_copy) if on_vector else (by_scalar, nc.scalar.copy)
-            if (g, h) == (1, 0):
-                make = handed_on
-            grouped = make([P, 2 * HALF], BF16, f"h_grouped{g}{h}{u}")
+        def group_h(g, h, u, who):
+            make, move = who
+            grouped = make([P, 4 * QUARTER], BF16, f"h_grouped{g}{h}{u}")
             move(
-                grouped[:].rearrange("p (c i t) -> p c t i", i=4, t=4),
-                h_planes[g, h][:, :, 256 * u : 256 * (u + 1)].rearrange("p t (c i) -> p c t i", i=4),
+                grouped[:].rearrange("p (e i t) -> p e t i", i=4, t=4),
+                h_rows[g, h][:, :, QUARTER * u : QUARTER * (u + 1)].rearrange("p t (e i) -> p e t i", i=4),
             )
             h_grouped[g, h, u] = grouped
 
         def group_h_on_gpsimd(g, h, u):
-            grouped = handed_on([P, 2 * HALF], BF16, f"h_grouped{g}{h}{u}")
+            grouped = handed_on([P, 4 * QUARTER], BF16, f"h_grouped{g}{h}{u}")
             nc.gpsimd.tensor_scalar(
-                grouped[:].rearrange("p (c t) -> p c t", t=4),
-                h_planes[g, h][:, :, 256 * u : 256 * (u + 1)].rearrange("p t c -> p c t"),
+                grouped[:].rearrange("p (e t) -> p e t", t=4),
+                h_rows[g, h][:, :, QUARTER * u : QUARTER * (u + 1)].rearrange("p t e -> p e t"),
                 1.0,
                 0.0,
                 ALU.mult,
@@ -255,35 +256,34 @@ def tile_list_routed_code_layer_kernel(
             codes = by_vector([P, HALF], U32, f"h_q{g}{h}")
             scales = held([P, HALF], U8, f"h_sc{g}{h}")
             for u in (1, 0):
-                cols = slice(256 * u, 256 * (u + 1))
+                cols = slice(QUARTER * u, QUARTER * (u + 1))
                 nc.vector.quantize_mx(out=codes[:, cols].bitcast(FP8X4), scales=scales[:, cols], in_=h_grouped[g, h, u][:])
             h_q[g, h] = codes, scales
 
         w1_grouped, w1_q = {}, {}
 
-        def group_w1(c, a, on_vector):
-            make, move = (by_vector, nc.vector.tensor_copy) if on_vector else (by_scalar, nc.scalar.copy)
-            src = w1_raw[c][:, a]
-            grouped = make([P, 4 * W1_COLS], BF16, f"w1_grouped{c}{a}")
+        def group_w1(c, g, who):
+            make, move = who
+            grouped = make([P, 4 * W1_COLS], BF16, f"w1_grouped{c}{g}")
             move(
-                grouped[:].rearrange("p (c i j) -> p c j i", i=4, j=4),
-                src.rearrange("p j (c i) -> p c j i", i=4),
+                grouped[:].rearrange("p (e i j) -> p e j i", i=4, j=4),
+                w1_raw[c][:, g].rearrange("p j (e i) -> p e j i", i=4),
             )
-            w1_grouped[c, a] = grouped
+            w1_grouped[c, g] = grouped
 
-        def quantise_w1(c, a):
-            w1_q[c, a] = quantised(w1_grouped[c, a], f"w1_q{c}{a}")
+        def quantise_w1(c, g):
+            w1_q[c, g] = quantised(w1_grouped[c, g], f"w1_q{c}{g}")
 
-        value, sig, gated = {}, {}, {}
+        value, sig, gated, resid = {}, {}, {}, {}
 
         def products(n, h):
-            c, m0 = divmod(P * n, W1_COLS)
+            c, col = divmod(P * n, W1_COLS)
             gate = psum.tile([P, HALF], F32, name="bank")
             for g in range(2):
                 nc.tensor.matmul_mx(
                     out=gate[:],
                     lhsT=w2_codes[:, g, P * n : P * (n + 1)].bitcast(FP8X4),
-                    lhsT_scale=w2_sc[:].bitcast(U8)[8 + 4 * g :, P * n : P * (n + 1)],
+                    lhsT_scale=w2_sc[:].bitcast(U8)[W2_SCALE_ROW + 4 * g :, P * n : P * (n + 1)],
                     rhs=h_q[g, h][0][:].bitcast(FP8X4),
                     rhs_scale=h_q[g, h][1][:],
                     start=(g == 0),
@@ -293,8 +293,8 @@ def tile_list_routed_code_layer_kernel(
             for g in range(2):
                 nc.tensor.matmul_mx(
                     out=value[n, h][:],
-                    lhsT=w1_q[c, g][0][:, m0 : m0 + P].bitcast(FP8X4),
-                    lhsT_scale=w1_q[c, g][1][:, m0 : m0 + P],
+                    lhsT=w1_q[c, g][0][:, col : col + P].bitcast(FP8X4),
+                    lhsT_scale=w1_q[c, g][1][:, col : col + P],
                     rhs=h_q[g, h][0][:].bitcast(FP8X4),
                     rhs_scale=h_q[g, h][1][:],
                     start=(g == 0),
@@ -307,32 +307,30 @@ def tile_list_routed_code_layer_kernel(
             gated[n, h] = by_vector([P, HALF], F32, f"gated{n}{h}")
             nc.vector.tensor_tensor(gated[n, h][:], value[n, h][:], sig[n, h][:], ALU.mult)
 
-        resid = {}
-
-        def residual(n, h):
+        def gather_residual(n, h):
             resid[n, h] = by_vector([P, HALF], F32, f"resid{n}{h}")
-            nc.vector.tensor_copy(resid[n, h][:], g_rows[n][:].indirect(offsets(idx, h)))
+            nc.vector.tensor_copy(resid[n, h][:], g_rows[n][:].indirect(offsets(idx, HALF * h, HALF)))
 
-        def add_residual(n, h, engine):
-            engine.tensor_tensor(gated[n, h][:], gated[n, h][:], resid[n, h][:], ALU.add)
+        def gate_add_store(n, h):
+            gate_value(n, h)
+            nc.gpsimd.tensor_tensor(gated[n, h][:], gated[n, h][:], resid[n, h][:], ALU.add)
             nc.sync.dma_start(out[P * n : P * (n + 1), HALF * h : HALF * (h + 1)], gated[n, h][:])
 
-        def finish(n, h, pieces=1):
+        def gather_add_store(n, h, pieces):
             width = HALF // pieces
-            for c0 in range(0, HALF, width):
-                j0 = HALF * h + c0
-                result = by_vector([P, width], F32, f"result{n}{h}{c0}")
-                picks = idx[:, j0 // 16 : (j0 + width) // 16]
-                nc.vector.tensor_tensor(result[:], g_rows[n][:].indirect(picks), gated[n, h][:, c0 : c0 + width], ALU.add)
-                nc.sync.dma_start(out[P * n : P * (n + 1), j0 : j0 + width], result[:])
-
+            for col in range(0, HALF, width):
+                first = HALF * h + col
+                result = by_vector([P, width], F32, f"result{n}{h}{col}")
+                picked = g_rows[n][:].indirect(offsets(idx, first, width))
+                nc.vector.tensor_tensor(result[:], picked, gated[n, h][:, col : col + width], ALU.add)
+                nc.sync.dma_start(out[P * n : P * (n + 1), first : first + width], result[:])
 
         for h in range(2):
             gather_code_scales(h)
         for h in range(2):
             gather_codes(h)
-        group_wa(0, 0, 0, False)
-        group_wa(0, 0, 1, False)
+        for u in range(2):
+            group_wa(0, 0, u, on_scalar)
         for h in range(2):
             gather_token_scales(h)
         quantise_wa(0, 0, 0)
@@ -341,96 +339,94 @@ def tile_list_routed_code_layer_kernel(
         token_passes(0, 0, 0)
         gather_tokens(0, 1)
         token_passes(0, 1, 0)
-        group_wa(0, 1, 0, False)
-        group_wa(0, 1, 1, False)
+        for u in range(2):
+            group_wa(0, 1, u, on_scalar)
         order_wb()
-        code_passes(0, 0)
-        code_passes(0, 1)
+        for h in range(2):
+            code_passes(0, h)
         quantise_wa(0, 1, 0)
         gather_tokens(1, 0)
         quantise_wa(0, 1, 1)
         token_passes(0, 0, 1)
         gather_tokens(1, 1)
         token_passes(0, 1, 1)
+
         empty_hidden(0, 0)
-        group_wa(1, 0, 0, True)
-        group_wa(1, 0, 1, True)
-        quantise_wa(1, 0, 0)
-        quantise_wa(1, 0, 1)
+        for u in range(2):
+            group_wa(1, 0, u, on_vector)
+        for u in range(2):
+            quantise_wa(1, 0, u)
         code_passes(1, 0)
         token_passes(1, 0, 0)
         empty_hidden(0, 1)
-        group_wa(1, 1, 0, True)
-        group_wa(1, 1, 1, True)
-        quantise_wa(1, 1, 0)
-        quantise_wa(1, 1, 1)
+        for u in range(2):
+            group_wa(1, 1, u, on_vector)
+        for u in range(2):
+            quantise_wa(1, 1, u)
         token_passes(1, 0, 1)
         token_passes(1, 1, 1)
         code_passes(1, 1)
         token_passes(1, 1, 0)
-        group_h(0, 0, 0, True)
-        group_h(0, 0, 1, True)
+
+        for u in range(2):
+            group_h(0, 0, u, on_vector)
         empty_hidden(1, 0)
-        group_w1(0, 0, True)
+        group_w1(0, 0, on_vector)
         quantise_h(0, 0)
-        group_w1(0, 1, False)
+        group_w1(0, 1, on_scalar)
         quantise_w1(0, 0)
-        group_h(1, 0, 0, True)
-        group_h(1, 0, 1, True)
+        for u in range(2):
+            group_h(1, 0, u, on_vector_handed_on)
         empty_hidden(1, 1)
         quantise_w1(0, 1)
         quantise_h(1, 0)
-        group_h_on_gpsimd(0, 1, 0)
-        group_h_on_gpsimd(0, 1, 1)
-        products(0, 0)
-        group_h(1, 1, 0, False)
-        products(1, 0)
-        group_h(1, 1, 1, False)
-        residual(0, 0)
-        residual(0, 1)
-        gate_value(0, 0)
-        add_residual(0, 0, nc.gpsimd)
-        residual(1, 0)
-        gate_value(1, 0)
-        quantise_h(0, 1)
-        quantise_h(1, 1)
-        add_residual(1, 0, nc.gpsimd)
-        group_w1(1, 0, False)
-        products(0, 1)
-        group_w1(1, 1, False)
-        products(1, 1)
-        residual(1, 1)
-        residual(2, 0)
-        gate_value(0, 1)
-        quantise_w1(1, 0)
-        quantise_w1(1, 1)
-        add_residual(0, 1, nc.gpsimd)
-        products(2, 0)
-        group_w1(2, 0, False)
-        products(2, 1)
-        group_w1(2, 1, False)
-        products(3, 0)
-        products(3, 1)
-        gate_value(1, 1)
-        add_residual(1, 1, nc.gpsimd)
-        residual(2, 1)
-        residual(3, 0)
-        gate_value(2, 0)
-        quantise_w1(2, 0)
-        quantise_w1(2, 1)
-        add_residual(2, 0, nc.gpsimd)
-        for n in (4, 5):
-            products(n, 0)
-            products(n, 1)
-        gate_value(2, 1)
-        add_residual(2, 1, nc.gpsimd)
-        residual(3, 1)
+
+        for u in range(2):
+            group_h_on_gpsimd(0, 1, u)
+        for step in range(2):
+            products(step, 0)
+            group_h(1, 1, step, on_scalar)
         for h in range(2):
-            gate_value(3, h)
-            add_residual(3, h, nc.gpsimd)
-        for n in (4, 5):
+            gather_residual(0, h)
+        gate_add_store(0, 0)
+        gather_residual(1, 0)
+        for g in range(2):
+            quantise_h(g, 1)
+
+        for g in range(2):
+            group_w1(1, g, on_scalar)
+        for n in range(2):
+            products(n, 1)
+        gate_add_store(1, 0)
+        gather_residual(1, 1)
+        gather_residual(2, 0)
+        for g in range(2):
+            quantise_w1(1, g)
+
+        for step in range(2):
+            group_w1(2, step, on_scalar)
+            products(2, step)
+        for h in range(2):
+            products(3, h)
+        gate_add_store(0, 1)
+        gather_residual(2, 1)
+        gate_add_store(1, 1)
+        gather_residual(3, 0)
+        for g in range(2):
+            quantise_w1(2, g)
+
+        last_two = (4, 5)
+        for n in last_two:
+            for h in range(2):
+                products(n, h)
+        gate_add_store(2, 0)
+        gather_residual(3, 1)
+        gate_add_store(2, 1)
+        for h in range(2):
+            gate_add_store(3, h)
+        for n in last_two:
             for h in range(2):
                 gate_value(n, h)
-        for n in (4, 5):
+        for n in last_two:
             for h in range(2):
-                finish(n, h, 2 if (n, h) == (5, 1) else 1)
+                gather_add_store(n, h, 2 if (n, h) == (last_two[-1], 1) else 1)

@@ -22,9 +22,9 @@ HALF = 512
 QUARTER = HALF // 2
 W1_COLS = 256
 W2_SCALE_ROW = 8
-LOAD_BUFS = 12
-VECTOR_BUFS = 37
-SCALAR_BUFS = 9
+LOAD_BUFS = 10
+VECTOR_BUFS = 42
+SCALAR_BUFS = 12
 
 
 def tile_list_routed_code_layer_kernel(
@@ -48,11 +48,7 @@ def tile_list_routed_code_layer_kernel(
         def by_scalar(shape, dtype, name):
             return ring.tile(shape, dtype, name=name, tag="by_scalar", bufs=SCALAR_BUFS, align_bytes=64)
 
-        def handed_on(shape, dtype, name):
-            return ring.tile(shape, dtype, name=name, tag="handed_on", bufs=2, align_bytes=64)
-
         on_vector = (by_vector, nc.vector.tensor_copy)
-        on_vector_handed_on = (handed_on, nc.vector.tensor_copy)
         on_scalar = (by_scalar, nc.scalar.copy)
 
         idx = keep.tile([P, S // 16], U16, name="idx")
@@ -62,7 +58,8 @@ def tile_list_routed_code_layer_kernel(
         wb_raw_scales = held([P, H // 4], I32, "wb_raw_scales")
         w2_sc = held([P, N // 4], I32, "w2_sc")
         wb_raw = held([P, H // 2], I32, "wb_raw")
-        w2_codes = held([P, 2, N], I32, "w2_codes")
+        w2_first = held([P, 2, W1_COLS], I32, "w2_first")
+        w2_rest = held([P, 2, N - W1_COLS], I32, "w2_rest")
         bias = held([P, 2, 4], F32, "bias")
         warm = held([P, 8], F32, "warm")
 
@@ -100,33 +97,41 @@ def tile_list_routed_code_layer_kernel(
                 nc.sync.dma_start(tile[:, g], rows.rearrange("(p j) m -> p j m", j=4))
             return tile
 
+        def load_w2(dst, first):
+            cols = w2_words[:, :, first : first + dst.shape[2], :]
+            nc.sync.dma_start(dst[:], cols.rearrange("g p e i -> p g (e i)").bitcast(I32))
+
         def load_g_rows(n):
             return load([P, T], F32, f"g_rows{n}", gT[P * n : P * (n + 1), :])
 
         wa_raw, tok_words, w1_raw, g_rows = {}, {}, {}, {}
         nc.sync.dma_start(idx2[:], offs2)
-        load_one_pass_scales(code_scales, tab2_scales)
         code_words = load_words(tab2_words[0], "code_words")
+        load_one_pass_scales(code_scales, tab2_scales)
         nc.sync.dma_start(idx[:], offs)
         wa_raw[0, 0] = load_wa(0, 0)
         nc.scalar.activation(warm[:, 4:8], warm[:, 0:4], ACT.Sigmoid)
-        load_two_pass_scales(tok_scales, tab_scales, 0)
-        tok_words[0] = load_words(tab_words[0], "tok_words0")
-        nc.sync.dma_start(wb_raw[:], wb_words[0].bitcast(I32))
-        wa_raw[0, 1] = load_wa(0, 1)
         load_one_pass_scales(wb_raw_scales, wb_scales)
+        nc.sync.dma_start(wb_raw[:], wb_words[0].bitcast(I32))
+        tok_words[0] = load_words(tab_words[0], "tok_words0")
+        load_two_pass_scales(tok_scales, tab_scales, 0)
+        wa_raw[0, 1] = load_wa(0, 1)
         tok_words[1] = load_words(tab_words[1], "tok_words1")
         nc.sync.dma_start(bias[:], b.rearrange("(g p t) -> p g t", p=P, t=4))
         wa_raw[1, 0] = load_wa(1, 0)
         wa_raw[1, 1] = load_wa(1, 1)
+        g_rows[0] = load_g_rows(0)
         w1_raw[0] = load_w1(0)
         load_two_pass_scales(w2_sc, w2_scales, W2_SCALE_ROW)
-        nc.sync.dma_start(w2_codes[:], w2_words.rearrange("g p e i -> p g (e i)").bitcast(I32))
-        g_rows[0] = load_g_rows(0)
-        for n in range(1, N // P):
+        load_w2(w2_first, 0)
+        g_rows[1] = load_g_rows(1)
+        w1_raw[1] = load_w1(1)
+        g_rows[2] = load_g_rows(2)
+        load_w2(w2_rest, W1_COLS)
+        g_rows[3] = load_g_rows(3)
+        w1_raw[2] = load_w1(2)
+        for n in range(4, N // P):
             g_rows[n] = load_g_rows(n)
-            if n < N // W1_COLS:
-                w1_raw[n] = load_w1(n)
 
         def offsets(lst, first, count):
             return lst[:, first // 16 : (first + count) // 16]
@@ -240,8 +245,7 @@ def tile_list_routed_code_layer_kernel(
             )
             h_grouped[g, h, u] = grouped
 
-        def group_h_on_gpsimd(g, h, u):
-            grouped = handed_on([P, 4 * QUARTER], BF16, f"h_grouped{g}{h}{u}")
+        def group_h_on_gpsimd(g, h, u, grouped):
             nc.gpsimd.tensor_scalar(
                 grouped[:].rearrange("p (e t) -> p e t", t=4),
                 h_rows[g, h][:, :, QUARTER * u : QUARTER * (u + 1)].rearrange("p t e -> p e t"),
@@ -262,39 +266,27 @@ def tile_list_routed_code_layer_kernel(
 
         w1_grouped, w1_q = {}, {}
 
-        def group_w1(c, g, who):
-            make, move = who
-            grouped = make([P, 4 * W1_COLS], BF16, f"w1_grouped{c}{g}")
-            move(
-                grouped[:].rearrange("p (e i j) -> p e j i", i=4, j=4),
+        def group_w1(c, g):
+            if g == 0:
+                w1_grouped[c] = by_scalar([P, 2 * 4 * W1_COLS], BF16, f"w1_grouped{c}")
+            nc.scalar.copy(
+                w1_grouped[c][:, 4 * W1_COLS * g : 4 * W1_COLS * (g + 1)].rearrange("p (e i j) -> p e j i", i=4, j=4),
                 w1_raw[c][:, g].rearrange("p j (e i) -> p e j i", i=4),
             )
-            w1_grouped[c, g] = grouped
 
-        def quantise_w1(c, g):
-            w1_q[c, g] = quantised(w1_grouped[c, g], f"w1_q{c}{g}")
+        def quantise_w1(c):
+            w1_q[c] = quantised(w1_grouped[c], f"w1_q{c}")
 
         value, sig, gated, resid = {}, {}, {}, {}
 
-        def products(n, h):
-            c, col = divmod(P * n, W1_COLS)
+        def gate_passes(n, h):
+            codes, col = (w2_first, P * n) if P * n < W1_COLS else (w2_rest, P * n - W1_COLS)
             gate = psum.tile([P, HALF], F32, name="bank")
             for g in range(2):
                 nc.tensor.matmul_mx(
                     out=gate[:],
-                    lhsT=w2_codes[:, g, P * n : P * (n + 1)].bitcast(FP8X4),
+                    lhsT=codes[:, g, col : col + P].bitcast(FP8X4),
                     lhsT_scale=w2_sc[:].bitcast(U8)[W2_SCALE_ROW + 4 * g :, P * n : P * (n + 1)],
-                    rhs=h_q[g, h][0][:].bitcast(FP8X4),
-                    rhs_scale=h_q[g, h][1][:],
-                    start=(g == 0),
-                    stop=(g == 1),
-                )
-            value[n, h] = psum.tile([P, HALF], F32, name="bank")
-            for g in range(2):
-                nc.tensor.matmul_mx(
-                    out=value[n, h][:],
-                    lhsT=w1_q[c, g][0][:, col : col + P].bitcast(FP8X4),
-                    lhsT_scale=w1_q[c, g][1][:, col : col + P],
                     rhs=h_q[g, h][0][:].bitcast(FP8X4),
                     rhs_scale=h_q[g, h][1][:],
                     start=(g == 0),
@@ -302,6 +294,24 @@ def tile_list_routed_code_layer_kernel(
                 )
             sig[n, h] = by_scalar([P, HALF], F32, f"sig{n}{h}")
             nc.scalar.activation(sig[n, h][:], gate[:], ACT.Sigmoid)
+
+        def value_passes(n, h):
+            c, col = divmod(P * n, W1_COLS)
+            value[n, h] = psum.tile([P, HALF], F32, name="bank")
+            for g in range(2):
+                nc.tensor.matmul_mx(
+                    out=value[n, h][:],
+                    lhsT=w1_q[c][0][:, W1_COLS * g + col : W1_COLS * g + col + P].bitcast(FP8X4),
+                    lhsT_scale=w1_q[c][1][:, W1_COLS * g + col : W1_COLS * g + col + P],
+                    rhs=h_q[g, h][0][:].bitcast(FP8X4),
+                    rhs_scale=h_q[g, h][1][:],
+                    start=(g == 0),
+                    stop=(g == 1),
+                )
+
+        def products(n, h):
+            gate_passes(n, h)
+            value_passes(n, h)
 
         def gate_value(n, h):
             gated[n, h] = by_vector([P, HALF], F32, f"gated{n}{h}")
@@ -311,10 +321,13 @@ def tile_list_routed_code_layer_kernel(
             resid[n, h] = by_vector([P, HALF], F32, f"resid{n}{h}")
             nc.vector.tensor_copy(resid[n, h][:], g_rows[n][:].indirect(offsets(idx, HALF * h, HALF)))
 
-        def gate_add_store(n, h):
-            gate_value(n, h)
-            nc.gpsimd.tensor_tensor(gated[n, h][:], gated[n, h][:], resid[n, h][:], ALU.add)
-            nc.sync.dma_start(out[P * n : P * (n + 1), HALF * h : HALF * (h + 1)], gated[n, h][:])
+        def spent_w1(c, half):
+            return w1_grouped[c][:].bitcast(F32)[:, HALF * half : HALF * (half + 1)]
+
+        def add_store(n, h, spent):
+            result = spent if spent is not None else gated[n, h][:]
+            nc.gpsimd.tensor_tensor(result, gated[n, h][:], resid[n, h][:], ALU.add)
+            nc.sync.dma_start(out[P * n : P * (n + 1), HALF * h : HALF * (h + 1)], result)
 
         def gather_add_store(n, h, pieces):
             width = HALF // pieces
@@ -326,24 +339,23 @@ def tile_list_routed_code_layer_kernel(
                 nc.sync.dma_start(out[P * n : P * (n + 1), first : first + width], result[:])
 
         for h in range(2):
-            gather_code_scales(h)
-        for h in range(2):
             gather_codes(h)
+        for h in range(2):
+            gather_code_scales(h)
         for u in range(2):
             group_wa(0, 0, u, on_scalar)
-        for h in range(2):
-            gather_token_scales(h)
-        quantise_wa(0, 0, 0)
-        gather_tokens(0, 0)
-        quantise_wa(0, 0, 1)
-        token_passes(0, 0, 0)
-        gather_tokens(0, 1)
-        token_passes(0, 1, 0)
-        for u in range(2):
-            group_wa(0, 1, u, on_scalar)
         order_wb()
         for h in range(2):
             code_passes(0, h)
+        for u in range(2):
+            quantise_wa(0, 0, u)
+        for h in range(2):
+            gather_tokens(0, h)
+        for h in range(2):
+            gather_token_scales(h)
+            token_passes(0, h, 0)
+        for u in range(2):
+            group_wa(0, 1, u, on_scalar)
         quantise_wa(0, 1, 0)
         gather_tokens(1, 0)
         quantise_wa(0, 1, 1)
@@ -368,65 +380,72 @@ def tile_list_routed_code_layer_kernel(
         code_passes(1, 1)
         token_passes(1, 1, 0)
 
-        for u in range(2):
-            group_h(0, 0, u, on_vector)
+        group_h(0, 0, 1, on_scalar)
+        for h in range(2):
+            group_h_on_gpsimd(0, h, h, wa_grouped[1, 1, h])
         empty_hidden(1, 0)
-        group_w1(0, 0, on_vector)
-        quantise_h(0, 0)
-        group_w1(0, 1, on_scalar)
-        quantise_w1(0, 0)
-        for u in range(2):
-            group_h(1, 0, u, on_vector_handed_on)
-        empty_hidden(1, 1)
-        quantise_w1(0, 1)
-        quantise_h(1, 0)
-
-        for u in range(2):
-            group_h_on_gpsimd(0, 1, u)
-        for step in range(2):
-            products(step, 0)
-            group_h(1, 1, step, on_scalar)
         for h in range(2):
             gather_residual(0, h)
-        gate_add_store(0, 0)
-        gather_residual(1, 0)
+        for u in range(2):
+            group_h(1, 0, u, on_vector)
         for g in range(2):
+            group_w1(0, g)
+        quantise_h(0, 0)
+        empty_hidden(1, 1)
+        quantise_w1(0)
+        quantise_h(1, 0)
+        spent = h_grouped[1, 0, 1], h_grouped[1, 0, 0]
+        group_h_on_gpsimd(0, 1, 0, spent[0])
+        group_h_on_gpsimd(1, 1, 0, spent[1])
+        for n in range(2):
+            gate_passes(n, 0)
+        for n in range(2):
+            value_passes(n, 0)
+        group_h(1, 1, 1, on_scalar)
+        for h in range(2):
+            gather_residual(1, h)
+        for n in range(2):
+            gate_value(n, 0)
+        for g in (1, 0):
             quantise_h(g, 1)
-
+        for n in range(2):
+            add_store(n, 0, h_grouped[0, 1, 1 - n][:].bitcast(F32))
         for g in range(2):
-            group_w1(1, g, on_scalar)
+            group_w1(1, g)
         for n in range(2):
             products(n, 1)
-        gate_add_store(1, 0)
-        gather_residual(1, 1)
-        gather_residual(2, 0)
-        for g in range(2):
-            quantise_w1(1, g)
-
-        for step in range(2):
-            group_w1(2, step, on_scalar)
-            products(2, step)
         for h in range(2):
-            products(3, h)
-        gate_add_store(0, 1)
-        gather_residual(2, 1)
-        gate_add_store(1, 1)
-        gather_residual(3, 0)
-        for g in range(2):
-            quantise_w1(2, g)
-
-        last_two = (4, 5)
-        for n in last_two:
+            gather_residual(2, h)
+        quantise_w1(1)
+        for n in range(2):
+            gate_value(n, 1)
+            add_store(n, 1, None)
+        for n in (2, 3):
             for h in range(2):
-                products(n, h)
-        gate_add_store(2, 0)
-        gather_residual(3, 1)
-        gate_add_store(2, 1)
+                gate_passes(n, h)
+            for h in range(2):
+                value_passes(n, h)
         for h in range(2):
-            gate_add_store(3, h)
-        for n in last_two:
+            gate_value(2, h)
+            add_store(2, h, None)
+        for g in range(2):
+            group_w1(2, g)
+        for h in range(2):
+            gather_residual(3, h)
+        for h in range(2):
+            gate_value(3, h)
+        for n in (4, 5):
             for h in range(2):
+                gate_passes(n, h)
+        quantise_w1(2)
+        for h in range(2):
+            add_store(3, h, spent_w1(2, h))
+        gather_residual(4, 0)
+        for n in (4, 5):
+            for h in range(2):
+                value_passes(n, h)
                 gate_value(n, h)
-        for n in last_two:
-            for h in range(2):
-                gather_add_store(n, h, 2 if (n, h) == (last_two[-1], 1) else 1)
+        add_store(4, 0, None)
+        gather_add_store(4, 1, 1)
+        for h in range(2):
+            gather_add_store(5, h, 1 + h)

@@ -22,9 +22,9 @@ HALF = 512
 QUARTER = HALF // 2
 W1_COLS = 256
 W2_SCALE_ROW = 8
-LOAD_BUFS = 10
-VECTOR_BUFS = 42
-SCALAR_BUFS = 12
+LOAD_BUFS = 9
+VECTOR_BUFS = 28
+SCALAR_BUFS = 8
 
 
 def tile_list_routed_code_layer_kernel(
@@ -48,8 +48,6 @@ def tile_list_routed_code_layer_kernel(
         def by_scalar(shape, dtype, name):
             return ring.tile(shape, dtype, name=name, tag="by_scalar", bufs=SCALAR_BUFS, align_bytes=64)
 
-        on_vector = (by_vector, nc.vector.tensor_copy)
-        on_scalar = (by_scalar, nc.scalar.copy)
 
         idx = keep.tile([P, S // 16], U16, name="idx")
         idx2 = keep.tile([P, S // 16], U16, name="idx2")
@@ -139,15 +137,15 @@ def tile_list_routed_code_layer_kernel(
         def gathered(window, lst, h, dtype, name):
             dst = by_vector([P, HALF], dtype, name)
             nc.vector.tensor_copy(dst[:], window[:].bitcast(dtype).indirect(offsets(lst, HALF * h, HALF)))
-            return dst
+            return dst[:]
 
-        c_sc, c_words, v_sc, v_words = {}, {}, {}, {}
+        def gathered_whole(window, lst, dtype, name):
+            dst = by_vector([P, S], dtype, name)
+            nc.vector.tensor_copy(dst[:], window[:].bitcast(dtype).indirect(lst[:]))
+            return dst[:, :HALF], dst[:, HALF:]
 
-        def gather_code_scales(h):
-            c_sc[h] = gathered(code_scales, idx2, h, U8, f"c_sc{h}")
+        v_sc, v_words = {}, {}
 
-        def gather_codes(h):
-            c_words[h] = gathered(code_words, idx2, h, U32, f"c_words{h}")
 
         def gather_token_scales(h):
             v_sc[h] = gathered(tok_scales, idx, h, U8, f"v_sc{h}")
@@ -173,16 +171,14 @@ def tile_list_routed_code_layer_kernel(
             cols = grouped.shape[1] // 4
             codes = by_vector([P, cols], U32, name)
             scales = held([P, cols], U8, name + "_sc")
-            nc.vector.quantize_mx(out=codes[:].bitcast(FP8X4), scales=scales[:], in_=grouped[:])
+            nc.vector.quantize_mx(out=codes[:].bitcast(FP8X4), scales=scales[:], in_=grouped)
             return codes, scales
 
         wa_grouped, wa_q = {}, {}
 
-        def group_wa(g, a, u, who):
-            make, move = who
-            grouped = make([P, 2 * PASS], BF16, f"wa_grouped{g}{a}{u}")
+        def group_wa(g, a, u, grouped, move):
             move(
-                grouped[:].rearrange("p (t m j) -> p m j t", t=2, j=4),
+                grouped.rearrange("p (t m j) -> p m j t", t=2, j=4),
                 wa_raw[g, a][:].rearrange("p j (m t) -> p m j t", t=4)[:, :, :, 2 * u : 2 * u + 2],
             )
             wa_grouped[g, a, u] = grouped
@@ -208,8 +204,8 @@ def tile_list_routed_code_layer_kernel(
                     out=acc[g, h, t][:],
                     lhsT=wb["codes"][:, 2 * col : 2 * (col + P)].bitcast(FP4X4),
                     lhsT_scale=wb["scales"][:, col : col + P],
-                    rhs=c_words[h][:].bitcast(FP8X4),
-                    rhs_scale=c_sc[h][:],
+                    rhs=c_words[h].bitcast(FP8X4),
+                    rhs_scale=c_sc[h],
                     start=first,
                     stop=last,
                 )
@@ -223,7 +219,7 @@ def tile_list_routed_code_layer_kernel(
                     out=acc[g, h, t][:],
                     lhsT=codes[:, cols].bitcast(FP8X4),
                     lhsT_scale=scales[:, cols],
-                    rhs=v_words[a, h][:].bitcast(FP8X4),
+                    rhs=v_words[a, h].bitcast(FP8X4),
                     rhs_scale=v_sc[h][4 * a :, :],
                     start=first,
                     stop=last,
@@ -236,33 +232,28 @@ def tile_list_routed_code_layer_kernel(
             for t in range(4):
                 nc.scalar.activation(h_rows[g, h][:, t, :], acc[g, h, t][:], ACT.Identity, bias=bias[:, g, t : t + 1])
 
-        def group_h(g, h, u, who):
-            make, move = who
-            grouped = make([P, 4 * QUARTER], BF16, f"h_grouped{g}{h}{u}")
+        def half_of(tile, u):
+            width = tile.shape[1] // 2
+            return tile[:, width * u : width * (u + 1)]
+
+        def group_h(g, h, u, move):
             move(
-                grouped[:].rearrange("p (e i t) -> p e t i", i=4, t=4),
+                half_of(h_grouped[g, h], u).rearrange("p (e i t) -> p e t i", i=4, t=4),
                 h_rows[g, h][:, :, QUARTER * u : QUARTER * (u + 1)].rearrange("p t (e i) -> p e t i", i=4),
             )
-            h_grouped[g, h, u] = grouped
 
-        def group_h_on_gpsimd(g, h, u, grouped):
+        def group_h_on_gpsimd(g, h, u):
             nc.gpsimd.tensor_scalar(
-                grouped[:].rearrange("p (e t) -> p e t", t=4),
+                half_of(h_grouped[g, h], u).rearrange("p (e t) -> p e t", t=4),
                 h_rows[g, h][:, :, QUARTER * u : QUARTER * (u + 1)].rearrange("p t e -> p e t"),
                 1.0,
                 0.0,
                 ALU.mult,
                 ALU.add,
             )
-            h_grouped[g, h, u] = grouped
 
         def quantise_h(g, h):
-            codes = by_vector([P, HALF], U32, f"h_q{g}{h}")
-            scales = held([P, HALF], U8, f"h_sc{g}{h}")
-            for u in (1, 0):
-                cols = slice(QUARTER * u, QUARTER * (u + 1))
-                nc.vector.quantize_mx(out=codes[:, cols].bitcast(FP8X4), scales=scales[:, cols], in_=h_grouped[g, h, u][:])
-            h_q[g, h] = codes, scales
+            h_q[g, h] = quantised(h_grouped[g, h][:], f"h_q{g}{h}")
 
         w1_grouped, w1_q = {}, {}
 
@@ -275,7 +266,7 @@ def tile_list_routed_code_layer_kernel(
             )
 
         def quantise_w1(c):
-            w1_q[c] = quantised(w1_grouped[c], f"w1_q{c}")
+            w1_q[c] = quantised(w1_grouped[c][:], f"w1_q{c}")
 
         value, sig, gated, resid = {}, {}, {}, {}
 
@@ -317,17 +308,15 @@ def tile_list_routed_code_layer_kernel(
             gated[n, h] = by_vector([P, HALF], F32, f"gated{n}{h}")
             nc.vector.tensor_tensor(gated[n, h][:], value[n, h][:], sig[n, h][:], ALU.mult)
 
-        def gather_residual(n, h):
-            resid[n, h] = by_vector([P, HALF], F32, f"resid{n}{h}")
-            nc.vector.tensor_copy(resid[n, h][:], g_rows[n][:].indirect(offsets(idx, HALF * h, HALF)))
+        def gather_residual(n):
+            resid[n] = by_vector([P, S], F32, f"resid{n}")
+            nc.vector.tensor_copy(resid[n][:], g_rows[n][:].indirect(idx[:]))
 
-        def spent_w1(c, half):
-            return w1_grouped[c][:].bitcast(F32)[:, HALF * half : HALF * (half + 1)]
+        def add_residual(n, h, rows):
+            nc.gpsimd.tensor_tensor(half_of(rows[:].bitcast(F32), h), gated[n, h][:], half_of(resid[n], h), ALU.add)
 
-        def add_store(n, h, spent):
-            result = spent if spent is not None else gated[n, h][:]
-            nc.gpsimd.tensor_tensor(result, gated[n, h][:], resid[n, h][:], ALU.add)
-            nc.sync.dma_start(out[P * n : P * (n + 1), HALF * h : HALF * (h + 1)], result)
+        def store_rows(n, rows):
+            nc.sync.dma_start(out[P * n : P * (n + 1), :], rows[:].bitcast(F32))
 
         def gather_add_store(n, h, pieces):
             width = HALF // pieces
@@ -338,24 +327,21 @@ def tile_list_routed_code_layer_kernel(
                 nc.vector.tensor_tensor(result[:], picked, gated[n, h][:, col : col + width], ALU.add)
                 nc.sync.dma_start(out[P * n : P * (n + 1), first : first + width], result[:])
 
-        for h in range(2):
-            gather_codes(h)
-        for h in range(2):
-            gather_code_scales(h)
+        c_words = gathered_whole(code_words, idx2, U32, "c_words")
+        c_sc = gathered_whole(code_scales, idx2, U8, "c_sc")
         for u in range(2):
-            group_wa(0, 0, u, on_scalar)
+            group_wa(0, 0, u, by_scalar([P, 2 * PASS], BF16, f"wa_grouped00{u}")[:], nc.scalar.copy)
         order_wb()
         for h in range(2):
             code_passes(0, h)
         for u in range(2):
             quantise_wa(0, 0, u)
-        for h in range(2):
-            gather_tokens(0, h)
+        v_words[0, 0], v_words[0, 1] = gathered_whole(tok_words[0], idx, U32, "v_words0")
         for h in range(2):
             gather_token_scales(h)
             token_passes(0, h, 0)
         for u in range(2):
-            group_wa(0, 1, u, on_scalar)
+            group_wa(0, 1, u, by_scalar([P, 2 * PASS], BF16, f"wa_grouped01{u}")[:], nc.scalar.copy)
         quantise_wa(0, 1, 0)
         gather_tokens(1, 0)
         quantise_wa(0, 1, 1)
@@ -364,15 +350,19 @@ def tile_list_routed_code_layer_kernel(
         token_passes(0, 1, 1)
 
         empty_hidden(0, 0)
+        wa10 = by_vector([P, 4 * PASS], BF16, "wa_grouped10")
         for u in range(2):
-            group_wa(1, 0, u, on_vector)
+            group_wa(1, 0, u, half_of(wa10, u), nc.vector.tensor_copy)
         for u in range(2):
             quantise_wa(1, 0, u)
         code_passes(1, 0)
         token_passes(1, 0, 0)
         empty_hidden(0, 1)
+        h_grouped[0, 0] = by_vector([P, 4 * HALF], BF16, "h_grouped00")
+        group_h(0, 0, 0, nc.vector.tensor_copy)
+        h_grouped[0, 1] = by_vector([P, 4 * HALF], BF16, "wa11_then_h01")
         for u in range(2):
-            group_wa(1, 1, u, on_vector)
+            group_wa(1, 1, u, half_of(h_grouped[0, 1], u), nc.vector.tensor_copy)
         for u in range(2):
             quantise_wa(1, 1, u)
         token_passes(1, 0, 1)
@@ -380,46 +370,44 @@ def tile_list_routed_code_layer_kernel(
         code_passes(1, 1)
         token_passes(1, 1, 0)
 
-        group_h(0, 0, 1, on_scalar)
-        for h in range(2):
-            group_h_on_gpsimd(0, h, h, wa_grouped[1, 1, h])
-        empty_hidden(1, 0)
-        for h in range(2):
-            gather_residual(0, h)
+        group_h(0, 0, 1, nc.scalar.copy)
         for u in range(2):
-            group_h(1, 0, u, on_vector)
+            group_h_on_gpsimd(0, 1, u)
+        empty_hidden(1, 0)
+        gather_residual(0)
+        h_grouped[1, 0] = h_grouped[1, 1] = by_vector([P, 4 * HALF], BF16, "h10_then_h11")
+        for u in range(2):
+            group_h(1, 0, u, nc.vector.tensor_copy)
         for g in range(2):
             group_w1(0, g)
-        quantise_h(0, 0)
+        for g in range(2):
+            quantise_h(g, 0)
         empty_hidden(1, 1)
         quantise_w1(0)
-        quantise_h(1, 0)
-        spent = h_grouped[1, 0, 1], h_grouped[1, 0, 0]
-        group_h_on_gpsimd(0, 1, 0, spent[0])
-        group_h_on_gpsimd(1, 1, 0, spent[1])
+        quantise_h(0, 1)
+        group_h_on_gpsimd(1, 1, 0)
         for n in range(2):
             gate_passes(n, 0)
         for n in range(2):
             value_passes(n, 0)
-        group_h(1, 1, 1, on_scalar)
-        for h in range(2):
-            gather_residual(1, h)
+        group_h(1, 1, 1, nc.scalar.copy)
+        gather_residual(1)
         for n in range(2):
             gate_value(n, 0)
-        for g in (1, 0):
-            quantise_h(g, 1)
+        quantise_h(1, 1)
+        rows = {0: h_grouped[1, 1], 1: resid[0], 2: resid[1]}
         for n in range(2):
-            add_store(n, 0, h_grouped[0, 1, 1 - n][:].bitcast(F32))
+            add_residual(n, 0, rows[n])
         for g in range(2):
             group_w1(1, g)
         for n in range(2):
             products(n, 1)
-        for h in range(2):
-            gather_residual(2, h)
+        gather_residual(2)
         quantise_w1(1)
         for n in range(2):
             gate_value(n, 1)
-            add_store(n, 1, None)
+            add_residual(n, 1, rows[n])
+            store_rows(n, rows[n])
         for n in (2, 3):
             for h in range(2):
                 gate_passes(n, h)
@@ -427,11 +415,11 @@ def tile_list_routed_code_layer_kernel(
                 value_passes(n, h)
         for h in range(2):
             gate_value(2, h)
-            add_store(2, h, None)
+            add_residual(2, h, rows[2])
+        store_rows(2, rows[2])
         for g in range(2):
             group_w1(2, g)
-        for h in range(2):
-            gather_residual(3, h)
+        gather_residual(3)
         for h in range(2):
             gate_value(3, h)
         for n in (4, 5):
@@ -439,13 +427,16 @@ def tile_list_routed_code_layer_kernel(
                 gate_passes(n, h)
         quantise_w1(2)
         for h in range(2):
-            add_store(3, h, spent_w1(2, h))
-        gather_residual(4, 0)
+            add_residual(3, h, w1_grouped[2])
+        store_rows(3, w1_grouped[2])
+        early = by_vector([P, HALF], F32, "resid40")
+        nc.vector.tensor_copy(early[:], g_rows[4][:].indirect(offsets(idx, 0, HALF)))
         for n in (4, 5):
             for h in range(2):
                 value_passes(n, h)
                 gate_value(n, h)
-        add_store(4, 0, None)
+        nc.gpsimd.tensor_tensor(gated[4, 0][:], gated[4, 0][:], early[:], ALU.add)
+        nc.sync.dma_start(out[P * 4 : P * 5, :HALF], gated[4, 0][:])
         gather_add_store(4, 1, 1)
         for h in range(2):
             gather_add_store(5, h, 1 + h)

@@ -48,7 +48,6 @@ def tile_list_routed_code_layer_kernel(
         def by_scalar(shape, dtype, name):
             return ring.tile(shape, dtype, name=name, tag="by_scalar", bufs=SCALAR_BUFS, align_bytes=64)
 
-
         idx = keep.tile([P, S // 16], U16, name="idx")
         idx2 = keep.tile([P, S // 16], U16, name="idx2")
         code_scales = held([P, T // 4], I32, "code_scales")
@@ -66,6 +65,8 @@ def tile_list_routed_code_layer_kernel(
         nc.vector.memset(warm[:, 0:4], 0.0)
         nc.vector.memset(wb_raw_scales[:], 0)
         nc.vector.memset(w2_sc[:], 0)
+
+        wa_raw, tok_words, w1_raw, g_rows = {}, {}, {}, {}
 
         def load(shape, dtype, name, src):
             tile = for_load(shape, dtype, name)
@@ -88,12 +89,11 @@ def tile_list_routed_code_layer_kernel(
             rows = wa[PASS * a : PASS * (a + 1), PASS * g : PASS * (g + 1)]
             return load([P, 4, PASS], F32, f"wa_raw{g}{a}", rows.rearrange("(p j) m -> p j m", j=4))
 
-        def load_w1(c):
-            tile = for_load([P, 2, 4, W1_COLS], F32, f"w1_raw{c}")
-            for g in range(2):
-                rows = w1[PASS * g : PASS * (g + 1), W1_COLS * c : W1_COLS * (c + 1)]
-                nc.sync.dma_start(tile[:, g], rows.rearrange("(p j) m -> p j m", j=4))
-            return tile
+        def load_w1(c, g):
+            if g == 0:
+                w1_raw[c] = for_load([P, 2, 4, W1_COLS], F32, f"w1_raw{c}")
+            rows = w1[PASS * g : PASS * (g + 1), W1_COLS * c : W1_COLS * (c + 1)]
+            nc.sync.dma_start(w1_raw[c][:, g], rows.rearrange("(p j) m -> p j m", j=4))
 
         def load_w2(dst, first):
             cols = w2_words[:, :, first : first + dst.shape[2], :]
@@ -102,7 +102,6 @@ def tile_list_routed_code_layer_kernel(
         def load_g_rows(n):
             return load([P, T], F32, f"g_rows{n}", gT[P * n : P * (n + 1), :])
 
-        wa_raw, tok_words, w1_raw, g_rows = {}, {}, {}, {}
         nc.sync.dma_start(idx2[:], offs2)
         code_words = load_words(tab2_words[0], "code_words")
         load_one_pass_scales(code_scales, tab2_scales)
@@ -119,24 +118,27 @@ def tile_list_routed_code_layer_kernel(
         wa_raw[1, 0] = load_wa(1, 0)
         wa_raw[1, 1] = load_wa(1, 1)
         g_rows[0] = load_g_rows(0)
-        w1_raw[0] = load_w1(0)
+        for g in range(2):
+            load_w1(0, g)
         load_two_pass_scales(w2_sc, w2_scales, W2_SCALE_ROW)
         load_w2(w2_first, 0)
         g_rows[1] = load_g_rows(1)
-        w1_raw[1] = load_w1(1)
+        load_w1(1, 0)
         g_rows[2] = load_g_rows(2)
+        load_w1(1, 1)
         load_w2(w2_rest, W1_COLS)
         g_rows[3] = load_g_rows(3)
-        w1_raw[2] = load_w1(2)
+        for g in range(2):
+            load_w1(2, g)
         for n in range(4, N // P):
             g_rows[n] = load_g_rows(n)
 
         def offsets(lst, first, count):
             return lst[:, first // 16 : (first + count) // 16]
 
-        def gathered(window, lst, h, dtype, name):
+        def gathered(window, lst, half, dtype, name):
             dst = by_vector([P, HALF], dtype, name)
-            nc.vector.tensor_copy(dst[:], window[:].bitcast(dtype).indirect(offsets(lst, HALF * h, HALF)))
+            nc.vector.tensor_copy(dst[:], window[:].bitcast(dtype).indirect(offsets(lst, HALF * half, HALF)))
             return dst[:]
 
         def gathered_whole(window, lst, dtype, name):
@@ -146,12 +148,11 @@ def tile_list_routed_code_layer_kernel(
 
         v_sc, v_words = {}, {}
 
+        def gather_token_scales(half):
+            v_sc[half] = gathered(tok_scales, idx, half, U8, f"v_sc{half}")
 
-        def gather_token_scales(h):
-            v_sc[h] = gathered(tok_scales, idx, h, U8, f"v_sc{h}")
-
-        def gather_tokens(a, h):
-            v_words[a, h] = gathered(tok_words[a], idx, h, U32, f"v_words{a}{h}")
+        def gather_tokens(a, half):
+            v_words[a, half] = gathered(tok_words[a], idx, half, U32, f"v_words{a}{half}")
 
         wb = {}
 
@@ -188,72 +189,72 @@ def tile_list_routed_code_layer_kernel(
 
         acc, runs_done = {}, {}
 
-        def next_run(g, h):
-            run = runs_done.get((g, h), 0)
-            runs_done[g, h] = run + 1
+        def next_run(g, half):
+            run = runs_done.get((g, half), 0)
+            runs_done[g, half] = run + 1
             if run == 0:
                 for t in range(4):
-                    acc[g, h, t] = psum.tile([P, HALF], F32, name="bank")
+                    acc[g, half, t] = psum.tile([P, HALF], F32, name="bank")
             return run == 0, run == 2
 
-        def code_passes(g, h):
-            first, last = next_run(g, h)
+        def code_passes(g, half):
+            first, last = next_run(g, half)
             for t in range(4):
                 col = PASS * g + P * t
                 nc.tensor.matmul_mx(
-                    out=acc[g, h, t][:],
+                    out=acc[g, half, t][:],
                     lhsT=wb["codes"][:, 2 * col : 2 * (col + P)].bitcast(FP4X4),
                     lhsT_scale=wb["scales"][:, col : col + P],
-                    rhs=c_words[h].bitcast(FP8X4),
-                    rhs_scale=c_sc[h],
+                    rhs=c_words[half].bitcast(FP8X4),
+                    rhs_scale=c_sc[half],
                     start=first,
                     stop=last,
                 )
 
-        def token_passes(g, h, a):
-            first, last = next_run(g, h)
+        def token_passes(g, half, a):
+            first, last = next_run(g, half)
             for t in range(4):
                 codes, scales = wa_q[g, a, t // 2]
                 cols = slice(P * (t % 2), P * (t % 2 + 1))
                 nc.tensor.matmul_mx(
-                    out=acc[g, h, t][:],
+                    out=acc[g, half, t][:],
                     lhsT=codes[:, cols].bitcast(FP8X4),
                     lhsT_scale=scales[:, cols],
-                    rhs=v_words[a, h].bitcast(FP8X4),
-                    rhs_scale=v_sc[h][4 * a :, :],
+                    rhs=v_words[a, half].bitcast(FP8X4),
+                    rhs_scale=v_sc[half][4 * a :, :],
                     start=first,
                     stop=last,
                 )
 
         h_rows, h_grouped, h_q = {}, {}, {}
 
-        def empty_hidden(g, h):
-            h_rows[g, h] = by_scalar([P, 4, HALF], BF16, f"h_rows{g}{h}")
+        def empty_hidden(g, half):
+            h_rows[g, half] = by_scalar([P, 4, HALF], BF16, f"h_rows{g}{half}")
             for t in range(4):
-                nc.scalar.activation(h_rows[g, h][:, t, :], acc[g, h, t][:], ACT.Identity, bias=bias[:, g, t : t + 1])
+                nc.scalar.activation(h_rows[g, half][:, t, :], acc[g, half, t][:], ACT.Identity, bias=bias[:, g, t : t + 1])
 
         def half_of(tile, u):
             width = tile.shape[1] // 2
             return tile[:, width * u : width * (u + 1)]
 
-        def group_h(g, h, u, move):
+        def group_h(g, half, u, move):
             move(
-                half_of(h_grouped[g, h], u).rearrange("p (e i t) -> p e t i", i=4, t=4),
-                h_rows[g, h][:, :, QUARTER * u : QUARTER * (u + 1)].rearrange("p t (e i) -> p e t i", i=4),
+                half_of(h_grouped[g, half], u).rearrange("p (e i t) -> p e t i", i=4, t=4),
+                h_rows[g, half][:, :, QUARTER * u : QUARTER * (u + 1)].rearrange("p t (e i) -> p e t i", i=4),
             )
 
-        def group_h_on_gpsimd(g, h, u):
+        def group_h_on_gpsimd(g, half, u):
             nc.gpsimd.tensor_scalar(
-                half_of(h_grouped[g, h], u).rearrange("p (e t) -> p e t", t=4),
-                h_rows[g, h][:, :, QUARTER * u : QUARTER * (u + 1)].rearrange("p t e -> p e t"),
+                half_of(h_grouped[g, half], u).rearrange("p (e t) -> p e t", t=4),
+                h_rows[g, half][:, :, QUARTER * u : QUARTER * (u + 1)].rearrange("p t e -> p e t"),
                 1.0,
                 0.0,
                 ALU.mult,
                 ALU.add,
             )
 
-        def quantise_h(g, h):
-            h_q[g, h] = quantised(h_grouped[g, h][:], f"h_q{g}{h}")
+        def quantise_h(g, half):
+            h_q[g, half] = quantised(h_grouped[g, half][:], f"h_q{g}{half}")
 
         w1_grouped, w1_q = {}, {}
 
@@ -270,7 +271,7 @@ def tile_list_routed_code_layer_kernel(
 
         value, sig, gated, resid = {}, {}, {}, {}
 
-        def gate_passes(n, h):
+        def gate_passes(n, half):
             codes, col = (w2_first, P * n) if P * n < W1_COLS else (w2_rest, P * n - W1_COLS)
             gate = psum.tile([P, HALF], F32, name="bank")
             for g in range(2):
@@ -278,53 +279,53 @@ def tile_list_routed_code_layer_kernel(
                     out=gate[:],
                     lhsT=codes[:, g, col : col + P].bitcast(FP8X4),
                     lhsT_scale=w2_sc[:].bitcast(U8)[W2_SCALE_ROW + 4 * g :, P * n : P * (n + 1)],
-                    rhs=h_q[g, h][0][:].bitcast(FP8X4),
-                    rhs_scale=h_q[g, h][1][:],
+                    rhs=h_q[g, half][0][:].bitcast(FP8X4),
+                    rhs_scale=h_q[g, half][1][:],
                     start=(g == 0),
                     stop=(g == 1),
                 )
-            sig[n, h] = by_scalar([P, HALF], F32, f"sig{n}{h}")
-            nc.scalar.activation(sig[n, h][:], gate[:], ACT.Sigmoid)
+            sig[n, half] = by_scalar([P, HALF], F32, f"sig{n}{half}")
+            nc.scalar.activation(sig[n, half][:], gate[:], ACT.Sigmoid)
 
-        def value_passes(n, h):
+        def value_passes(n, half):
             c, col = divmod(P * n, W1_COLS)
-            value[n, h] = psum.tile([P, HALF], F32, name="bank")
+            value[n, half] = psum.tile([P, HALF], F32, name="bank")
             for g in range(2):
                 nc.tensor.matmul_mx(
-                    out=value[n, h][:],
+                    out=value[n, half][:],
                     lhsT=w1_q[c][0][:, W1_COLS * g + col : W1_COLS * g + col + P].bitcast(FP8X4),
                     lhsT_scale=w1_q[c][1][:, W1_COLS * g + col : W1_COLS * g + col + P],
-                    rhs=h_q[g, h][0][:].bitcast(FP8X4),
-                    rhs_scale=h_q[g, h][1][:],
+                    rhs=h_q[g, half][0][:].bitcast(FP8X4),
+                    rhs_scale=h_q[g, half][1][:],
                     start=(g == 0),
                     stop=(g == 1),
                 )
 
-        def products(n, h):
-            gate_passes(n, h)
-            value_passes(n, h)
+        def products(n, half):
+            gate_passes(n, half)
+            value_passes(n, half)
 
-        def gate_value(n, h):
-            gated[n, h] = by_vector([P, HALF], F32, f"gated{n}{h}")
-            nc.vector.tensor_tensor(gated[n, h][:], value[n, h][:], sig[n, h][:], ALU.mult)
+        def gate_value(n, half):
+            gated[n, half] = by_vector([P, HALF], F32, f"gated{n}{half}")
+            nc.vector.tensor_tensor(gated[n, half][:], value[n, half][:], sig[n, half][:], ALU.mult)
 
         def gather_residual(n):
             resid[n] = by_vector([P, S], F32, f"resid{n}")
             nc.vector.tensor_copy(resid[n][:], g_rows[n][:].indirect(idx[:]))
 
-        def add_residual(n, h, rows):
-            nc.gpsimd.tensor_tensor(half_of(rows[:].bitcast(F32), h), gated[n, h][:], half_of(resid[n], h), ALU.add)
+        def add_residual(n, half, rows):
+            nc.gpsimd.tensor_tensor(half_of(rows[:].bitcast(F32), half), gated[n, half][:], half_of(resid[n], half), ALU.add)
 
         def store_rows(n, rows):
             nc.sync.dma_start(out[P * n : P * (n + 1), :], rows[:].bitcast(F32))
 
-        def gather_add_store(n, h, pieces):
+        def gather_add_store(n, half, pieces):
             width = HALF // pieces
             for col in range(0, HALF, width):
-                first = HALF * h + col
-                result = by_vector([P, width], F32, f"result{n}{h}{col}")
+                first = HALF * half + col
+                result = by_vector([P, width], F32, f"result{n}{half}{col}")
                 picked = g_rows[n][:].indirect(offsets(idx, first, width))
-                nc.vector.tensor_tensor(result[:], picked, gated[n, h][:, col : col + width], ALU.add)
+                nc.vector.tensor_tensor(result[:], picked, gated[n, half][:, col : col + width], ALU.add)
                 nc.sync.dma_start(out[P * n : P * (n + 1), first : first + width], result[:])
 
         c_words = gathered_whole(code_words, idx2, U32, "c_words")
@@ -332,14 +333,14 @@ def tile_list_routed_code_layer_kernel(
         for u in range(2):
             group_wa(0, 0, u, by_scalar([P, 2 * PASS], BF16, f"wa_grouped00{u}")[:], nc.scalar.copy)
         order_wb()
-        for h in range(2):
-            code_passes(0, h)
+        for half in range(2):
+            code_passes(0, half)
         for u in range(2):
             quantise_wa(0, 0, u)
         v_words[0, 0], v_words[0, 1] = gathered_whole(tok_words[0], idx, U32, "v_words0")
-        for h in range(2):
-            gather_token_scales(h)
-            token_passes(0, h, 0)
+        for half in range(2):
+            gather_token_scales(half)
+            token_passes(0, half, 0)
         for u in range(2):
             group_wa(0, 1, u, by_scalar([P, 2 * PASS], BF16, f"wa_grouped01{u}")[:], nc.scalar.copy)
         quantise_wa(0, 1, 0)
@@ -350,9 +351,9 @@ def tile_list_routed_code_layer_kernel(
         token_passes(0, 1, 1)
 
         empty_hidden(0, 0)
-        wa10 = by_vector([P, 4 * PASS], BF16, "wa_grouped10")
+        wa_grouped10 = by_vector([P, 4 * PASS], BF16, "wa_grouped10")
         for u in range(2):
-            group_wa(1, 0, u, half_of(wa10, u), nc.vector.tensor_copy)
+            group_wa(1, 0, u, half_of(wa_grouped10, u), nc.vector.tensor_copy)
         for u in range(2):
             quantise_wa(1, 0, u)
         code_passes(1, 0)
@@ -386,18 +387,19 @@ def tile_list_routed_code_layer_kernel(
         quantise_w1(0)
         quantise_h(0, 1)
         group_h_on_gpsimd(1, 1, 0)
+        group_h(1, 1, 1, nc.scalar.copy)
+
         for n in range(2):
             gate_passes(n, 0)
         for n in range(2):
             value_passes(n, 0)
-        group_h(1, 1, 1, nc.scalar.copy)
         gather_residual(1)
+        quantise_h(1, 1)
         for n in range(2):
             gate_value(n, 0)
-        quantise_h(1, 1)
-        rows = {0: h_grouped[1, 1], 1: resid[0], 2: resid[1]}
+        finished = [h_grouped[1, 1], resid[0], resid[1]]
         for n in range(2):
-            add_residual(n, 0, rows[n])
+            add_residual(n, 0, finished[n])
         for g in range(2):
             group_w1(1, g)
         for n in range(2):
@@ -406,37 +408,38 @@ def tile_list_routed_code_layer_kernel(
         quantise_w1(1)
         for n in range(2):
             gate_value(n, 1)
-            add_residual(n, 1, rows[n])
-            store_rows(n, rows[n])
+            add_residual(n, 1, finished[n])
+            store_rows(n, finished[n])
+
         for n in (2, 3):
-            for h in range(2):
-                gate_passes(n, h)
-            for h in range(2):
-                value_passes(n, h)
-        for h in range(2):
-            gate_value(2, h)
-            add_residual(2, h, rows[2])
-        store_rows(2, rows[2])
+            for half in range(2):
+                gate_passes(n, half)
+            for half in range(2):
+                value_passes(n, half)
+        for half in range(2):
+            gate_value(2, half)
+            add_residual(2, half, finished[2])
+        store_rows(2, finished[2])
         for g in range(2):
             group_w1(2, g)
         gather_residual(3)
-        for h in range(2):
-            gate_value(3, h)
+        for half in range(2):
+            gate_value(3, half)
+
         for n in (4, 5):
-            for h in range(2):
-                gate_passes(n, h)
+            for half in range(2):
+                gate_passes(n, half)
         quantise_w1(2)
-        for h in range(2):
-            add_residual(3, h, w1_grouped[2])
+        for half in range(2):
+            add_residual(3, half, w1_grouped[2])
         store_rows(3, w1_grouped[2])
-        early = by_vector([P, HALF], F32, "resid40")
-        nc.vector.tensor_copy(early[:], g_rows[4][:].indirect(offsets(idx, 0, HALF)))
+        resid_40 = gathered(g_rows[4], idx, 0, F32, "resid40")
         for n in (4, 5):
-            for h in range(2):
-                value_passes(n, h)
-                gate_value(n, h)
-        nc.gpsimd.tensor_tensor(gated[4, 0][:], gated[4, 0][:], early[:], ALU.add)
+            for half in range(2):
+                value_passes(n, half)
+                gate_value(n, half)
+        nc.gpsimd.tensor_tensor(gated[4, 0][:], gated[4, 0][:], resid_40, ALU.add)
         nc.sync.dma_start(out[P * 4 : P * 5, :HALF], gated[4, 0][:])
         gather_add_store(4, 1, 1)
-        for h in range(2):
-            gather_add_store(5, h, 1 + h)
+        gather_add_store(5, 0, 1)
+        gather_add_store(5, 1, 2)

@@ -23,7 +23,7 @@ QUARTER = HALF // 2
 W1_COLS = 256
 W2_SCALE_ROW = 8
 LOAD_BUFS = 9
-VECTOR_BUFS = 28
+VECTOR_BUFS = 27
 SCALAR_BUFS = 8
 
 
@@ -37,16 +37,16 @@ def tile_list_routed_code_layer_kernel(
         psum = ctx.enter_context(tc.psum_pool(name="psum", bufs=8))
 
         def held(shape, dtype, name):
-            return keep.tile(shape, dtype, name=name, align_bytes=64)
+            return keep.tile(shape, dtype, name=name, align_bytes=256)
 
         def for_load(shape, dtype, name):
-            return ring.tile(shape, dtype, name=name, tag="loaded", bufs=LOAD_BUFS, align_bytes=64)
+            return ring.tile(shape, dtype, name=name, tag="loaded", bufs=LOAD_BUFS, align_bytes=256)
 
         def by_vector(shape, dtype, name):
-            return ring.tile(shape, dtype, name=name, tag="by_vector", bufs=VECTOR_BUFS, align_bytes=64)
+            return ring.tile(shape, dtype, name=name, tag="by_vector", bufs=VECTOR_BUFS, align_bytes=256)
 
         def by_scalar(shape, dtype, name):
-            return ring.tile(shape, dtype, name=name, tag="by_scalar", bufs=SCALAR_BUFS, align_bytes=64)
+            return ring.tile(shape, dtype, name=name, tag="by_scalar", bufs=SCALAR_BUFS, align_bytes=256)
 
         idx = keep.tile([P, S // 16], U16, name="idx")
         idx2 = keep.tile([P, S // 16], U16, name="idx2")
@@ -81,7 +81,7 @@ def tile_list_routed_code_layer_kernel(
                 nc.sync.dma_start(dst[r:P:32, :], src[0, r:16:4, :].bitcast(I32))
 
         def load_two_pass_scales(dst, src, first_row):
-            for quad in range(4):
+            for quad in (0, 2, 1, 3):
                 p0 = 32 * quad + first_row
                 nc.sync.dma_start(dst[p0 : p0 + 8, :], src[:, 4 * quad : 4 * quad + 4, :].bitcast(I32))
 
@@ -111,7 +111,7 @@ def tile_list_routed_code_layer_kernel(
         load_one_pass_scales(wb_raw_scales, wb_scales)
         nc.sync.dma_start(wb_raw[:], wb_words[0].bitcast(I32))
         tok_words[0] = load_words(tab_words[0], "tok_words0")
-        load_two_pass_scales(tok_scales, tab_scales, 0)
+        load_two_pass_scales(tok_scales, tab_scales, 8)
         wa_raw[0, 1] = load_wa(0, 1)
         tok_words[1] = load_words(tab_words[1], "tok_words1")
         nc.sync.dma_start(bias[:], b.rearrange("(g p t) -> p g t", p=P, t=4))
@@ -221,7 +221,7 @@ def tile_list_routed_code_layer_kernel(
                     lhsT=codes[:, cols].bitcast(FP8X4),
                     lhsT_scale=scales[:, cols],
                     rhs=v_words[a, half].bitcast(FP8X4),
-                    rhs_scale=v_sc[half][4 * a :, :],
+                    rhs_scale=v_sc[half][8 + 4 * a :, :],
                     start=first,
                     stop=last,
                 )

from contextlib import ExitStack

import concourse.mybir as mybir

K, K2, H, N, T, S = 1024, 512, 1024, 768, 2048, 1024
FLOPS = 2 * S * (K * H + K2 * H + 2 * H * N)

F32 = mybir.dt.float32
BF16 = mybir.dt.bfloat16
I32 = mybir.dt.int32
U32 = mybir.dt.uint32
U16 = mybir.dt.uint16
U8 = mybir.dt.uint8
FP8X4 = mybir.dt.float8_e4m3fn_x4
FP4X4 = mybir.dt.float4_e2m1fn_x4
ACT = mybir.ActivationFunctionType
ALU = mybir.AluOpType

P = 128
PASS = 512
HALF = 512
QUARTER = HALF // 2
W1_COLS = 256
W2_SCALE_ROW = 8
LOAD_BUFS = 9
VECTOR_BUFS = 27
SCALAR_BUFS = 8


def tile_list_routed_code_layer_kernel(
    tc, tab_words, tab_scales, tab2_words, tab2_scales, offs, offs2, wa, wb_words, wb_scales, b, w1, w2_words, w2_scales, gT, out
):
    nc = tc.nc
    with ExitStack() as ctx:
        keep = ctx.enter_context(tc.tile_pool(name="keep", bufs=1))
        ring = ctx.enter_context(tc.tile_pool(name="ring", bufs=2))
        psum = ctx.enter_context(tc.psum_pool(name="psum", bufs=8))

        def held(shape, dtype, name):
            return keep.tile(shape, dtype, name=name, align_bytes=256)

        def for_load(shape, dtype, name):
            return ring.tile(shape, dtype, name=name, tag="loaded", bufs=LOAD_BUFS, align_bytes=256)

        def by_vector(shape, dtype, name):
            return ring.tile(shape, dtype, name=name, tag="by_vector", bufs=VECTOR_BUFS, align_bytes=256)

        def by_scalar(shape, dtype, name):
            return ring.tile(shape, dtype, name=name, tag="by_scalar", bufs=SCALAR_BUFS, align_bytes=256)

        idx = keep.tile([P, S // 16], U16, name="idx")
        idx2 = keep.tile([P, S // 16], U16, name="idx2")
        code_scales = held([P, T // 4], I32, "code_scales")
        tok_scales = held([P, T // 4], I32, "tok_scales")
        wb_raw_scales = held([P, H // 4], I32, "wb_raw_scales")
        w2_sc = held([P, N // 4], I32, "w2_sc")
        wb_raw = held([P, H // 2], I32, "wb_raw")
        w2_first = held([P, 2, W1_COLS], I32, "w2_first")
        w2_rest = held([P, 2, N - W1_COLS], I32, "w2_rest")
        bias = held([P, 2, 4], F32, "bias")
        warm = held([P, 8], F32, "warm")

        nc.vector.memset(code_scales[:], 0)
        nc.vector.memset(tok_scales[:], 0)
        nc.vector.memset(warm[:, 0:4], 0.0)
        nc.vector.memset(wb_raw_scales[:], 0)
        nc.vector.memset(w2_sc[:], 0)

        wa_raw, tok_words, w1_raw, g_rows = {}, {}, {}, {}

        def load(shape, dtype, name, src):
            tile = for_load(shape, dtype, name)
            nc.sync.dma_start(tile[:], src)
            return tile

        def load_words(table_pass, name):
            return load([P, T], I32, name, table_pass.rearrange("p t i -> p (t i)").bitcast(I32))

        def load_one_pass_scales(dst, src):
            for r in range(4):
                nc.sync.dma_start(dst[r:P:32, :], src[0, r:16:4, :].bitcast(I32))

        def load_two_pass_scales(dst, src, first_row):
            for quad in (0, 2, 1, 3):
                p0 = 32 * quad + first_row
                nc.sync.dma_start(dst[p0 : p0 + 8, :], src[:, 4 * quad : 4 * quad + 4, :].bitcast(I32))

        def load_wa(g, a):
            rows = wa[PASS * a : PASS * (a + 1), PASS * g : PASS * (g + 1)]
            return load([P, 4, PASS], F32, f"wa_raw{g}{a}", rows.rearrange("(p j) m -> p j m", j=4))

        def load_w1(c, g):
            if g == 0:
                w1_raw[c] = for_load([P, 2, 4, W1_COLS], F32, f"w1_raw{c}")
            rows = w1[PASS * g : PASS * (g + 1), W1_COLS * c : W1_COLS * (c + 1)]
            nc.sync.dma_start(w1_raw[c][:, g], rows.rearrange("(p j) m -> p j m", j=4))

        def load_w2(dst, first):
            cols = w2_words[:, :, first : first + dst.shape[2], :]
            nc.sync.dma_start(dst[:], cols.rearrange("g p e i -> p g (e i)").bitcast(I32))

        def load_g_rows(n):
            return load([P, T], F32, f"g_rows{n}", gT[P * n : P * (n + 1), :])

        nc.sync.dma_start(idx2[:], offs2)
        code_words = load_words(tab2_words[0], "code_words")
        load_one_pass_scales(code_scales, tab2_scales)
        nc.sync.dma_start(idx[:], offs)
        wa_raw[0, 0] = load_wa(0, 0)
        nc.scalar.activation(warm[:, 4:8], warm[:, 0:4], ACT.Sigmoid)
        load_one_pass_scales(wb_raw_scales, wb_scales)
        nc.sync.dma_start(wb_raw[:], wb_words[0].bitcast(I32))
        tok_words[0] = load_words(tab_words[0], "tok_words0")
        load_two_pass_scales(tok_scales, tab_scales, 8)
        wa_raw[0, 1] = load_wa(0, 1)
        tok_words[1] = load_words(tab_words[1], "tok_words1")
        nc.sync.dma_start(bias[:], b.rearrange("(g p t) -> p g t", p=P, t=4))
        wa_raw[1, 0] = load_wa(1, 0)
        wa_raw[1, 1] = load_wa(1, 1)
        g_rows[0] = load_g_rows(0)
        for g in range(2):
            load_w1(0, g)
        load_two_pass_scales(w2_sc, w2_scales, W2_SCALE_ROW)
        load_w2(w2_first, 0)
        g_rows[1] = load_g_rows(1)
        load_w1(1, 0)
        g_rows[2] = load_g_rows(2)
        load_w1(1, 1)
        load_w2(w2_rest, W1_COLS)
        g_rows[3] = load_g_rows(3)
        for g in range(2):
            load_w1(2, g)
        for n in range(4, N // P):
            g_rows[n] = load_g_rows(n)

        def offsets(lst, first, count):
            return lst[:, first // 16 : (first + count) // 16]

        def gathered(window, lst, half, dtype, name):
            dst = by_vector([P, HALF], dtype, name)
            nc.vector.tensor_copy(dst[:], window[:].bitcast(dtype).indirect(offsets(lst, HALF * half, HALF)))
            return dst[:]

        def gathered_whole(window, lst, dtype, name):
            dst = by_vector([P, S], dtype, name)
            nc.vector.tensor_copy(dst[:], window[:].bitcast(dtype).indirect(lst[:]))
            return dst[:, :HALF], dst[:, HALF:]

        v_sc, v_words = {}, {}

        def gather_token_scales(half):
            v_sc[half] = gathered(tok_scales, idx, half, U8, f"v_sc{half}")

        def gather_tokens(a, half):
            v_words[a, half] = gathered(tok_words[a], idx, half, U32, f"v_words{a}{half}")

        wb = {}

        def order_wb():
            wb["codes"] = by_vector([P, 2 * H], U8, "wb_codes")
            nc.vector.tensor_copy(
                wb["codes"][:].bitcast(U16).rearrange("p (g t m) -> p g t m", g=2, t=4),
                wb_raw[:].bitcast(U16).rearrange("p (g m t) -> p g t m", g=2, t=4),
            )
            wb["scales"] = by_vector([P, H], U8, "wb_sc")
            nc.vector.tensor_copy(
                wb["scales"][:].rearrange("p (g t m) -> p g t m", g=2, t=4),
                wb_raw_scales[:].bitcast(U8).rearrange("p (g m t) -> p g t m", g=2, t=4),
            )

        def quantised(grouped, name):
            cols = grouped.shape[1] // 4
            codes = by_vector([P, cols], U32, name)
            scales = held([P, cols], U8, name + "_sc")
            nc.vector.quantize_mx(out=codes[:].bitcast(FP8X4), scales=scales[:], in_=grouped)
            return codes, scales

        wa_grouped, wa_q = {}, {}

        def group_wa(g, a, u, grouped, move):
            move(
                grouped.rearrange("p (t m j) -> p m j t", t=2, j=4),
                wa_raw[g, a][:].rearrange("p j (m t) -> p m j t", t=4)[:, :, :, 2 * u : 2 * u + 2],
            )
            wa_grouped[g, a, u] = grouped

        def quantise_wa(g, a, u):
            wa_q[g, a, u] = quantised(wa_grouped[g, a, u], f"wa_q{g}{a}{u}")

        acc, runs_done = {}, {}

        def next_run(g, half):
            run = runs_done.get((g, half), 0)
            runs_done[g, half] = run + 1
            if run == 0:
                for t in range(4):
                    acc[g, half, t] = psum.tile([P, HALF], F32, name="bank")
            return run == 0, run == 2

        def code_passes(g, half):
            first, last = next_run(g, half)
            for t in range(4):
                col = PASS * g + P * t
                nc.tensor.matmul_mx(
                    out=acc[g, half, t][:],
                    lhsT=wb["codes"][:, 2 * col : 2 * (col + P)].bitcast(FP4X4),
                    lhsT_scale=wb["scales"][:, col : col + P],
                    rhs=c_words[half].bitcast(FP8X4),
                    rhs_scale=c_sc[half],
                    start=first,
                    stop=last,
                )

        def token_passes(g, half, a):
            first, last = next_run(g, half)
            for t in range(4):
                codes, scales = wa_q[g, a, t // 2]
                cols = slice(P * (t % 2), P * (t % 2 + 1))
                nc.tensor.matmul_mx(
                    out=acc[g, half, t][:],
                    lhsT=codes[:, cols].bitcast(FP8X4),
                    lhsT_scale=scales[:, cols],
                    rhs=v_words[a, half].bitcast(FP8X4),
                    rhs_scale=v_sc[half][8 + 4 * a :, :],
                    start=first,
                    stop=last,
                )

        h_rows, h_grouped, h_q = {}, {}, {}

        def empty_hidden(g, half):
            h_rows[g, half] = by_scalar([P, 4, HALF], BF16, f"h_rows{g}{half}")
            for t in range(4):
                nc.scalar.activation(h_rows[g, half][:, t, :], acc[g, half, t][:], ACT.Identity, bias=bias[:, g, t : t + 1])

        def half_of(tile, u):
            width = tile.shape[1] // 2
            return tile[:, width * u : width * (u + 1)]

        def group_h(g, half, u, move):
            move(
                half_of(h_grouped[g, half], u).rearrange("p (e i t) -> p e t i", i=4, t=4),
                h_rows[g, half][:, :, QUARTER * u : QUARTER * (u + 1)].rearrange("p t (e i) -> p e t i", i=4),
            )

        def group_h_on_gpsimd(g, half, u):
            nc.gpsimd.tensor_scalar(
                half_of(h_grouped[g, half], u).rearrange("p (e t) -> p e t", t=4),
                h_rows[g, half][:, :, QUARTER * u : QUARTER * (u + 1)].rearrange("p t e -> p e t"),
                1.0,
                0.0,
                ALU.mult,
                ALU.add,
            )

        def quantise_h(g, half):
            h_q[g, half] = quantised(h_grouped[g, half][:], f"h_q{g}{half}")

        w1_grouped, w1_q = {}, {}

        def group_w1(c, g):
            if g == 0:
                w1_grouped[c] = by_scalar([P, 2 * 4 * W1_COLS], BF16, f"w1_grouped{c}")
            nc.scalar.copy(
                w1_grouped[c][:, 4 * W1_COLS * g : 4 * W1_COLS * (g + 1)].rearrange("p (e i j) -> p e j i", i=4, j=4),
                w1_raw[c][:, g].rearrange("p j (e i) -> p e j i", i=4),
            )

        def quantise_w1(c):
            w1_q[c] = quantised(w1_grouped[c][:], f"w1_q{c}")

        value, sig, gated, resid = {}, {}, {}, {}

        def gate_passes(n, half):
            codes, col = (w2_first, P * n) if P * n < W1_COLS else (w2_rest, P * n - W1_COLS)
            gate = psum.tile([P, HALF], F32, name="bank")
            for g in range(2):
                nc.tensor.matmul_mx(
                    out=gate[:],
                    lhsT=codes[:, g, col : col + P].bitcast(FP8X4),
                    lhsT_scale=w2_sc[:].bitcast(U8)[W2_SCALE_ROW + 4 * g :, P * n : P * (n + 1)],
                    rhs=h_q[g, half][0][:].bitcast(FP8X4),
                    rhs_scale=h_q[g, half][1][:],
                    start=(g == 0),
                    stop=(g == 1),
                )
            sig[n, half] = by_scalar([P, HALF], F32, f"sig{n}{half}")
            nc.scalar.activation(sig[n, half][:], gate[:], ACT.Sigmoid)

        def value_passes(n, half):
            c, col = divmod(P * n, W1_COLS)
            value[n, half] = psum.tile([P, HALF], F32, name="bank")
            for g in range(2):
                nc.tensor.matmul_mx(
                    out=value[n, half][:],
                    lhsT=w1_q[c][0][:, W1_COLS * g + col : W1_COLS * g + col + P].bitcast(FP8X4),
                    lhsT_scale=w1_q[c][1][:, W1_COLS * g + col : W1_COLS * g + col + P],
                    rhs=h_q[g, half][0][:].bitcast(FP8X4),
                    rhs_scale=h_q[g, half][1][:],
                    start=(g == 0),
                    stop=(g == 1),
                )

        def products(n, half):
            gate_passes(n, half)
            value_passes(n, half)

        def gate_value(n, half):
            gated[n, half] = by_vector([P, HALF], F32, f"gated{n}{half}")
            nc.vector.tensor_tensor(gated[n, half][:], value[n, half][:], sig[n, half][:], ALU.mult)

        def gather_residual(n):
            resid[n] = by_vector([P, S], F32, f"resid{n}")
            nc.vector.tensor_copy(resid[n][:], g_rows[n][:].indirect(idx[:]))

        def add_residual(n, half, rows):
            nc.gpsimd.tensor_tensor(half_of(rows[:].bitcast(F32), half), gated[n, half][:], half_of(resid[n], half), ALU.add)

        def store_rows(n, rows):
            nc.sync.dma_start(out[P * n : P * (n + 1), :], rows[:].bitcast(F32))

        def gather_add_store(n, half, pieces):
            width = HALF // pieces
            for col in range(0, HALF, width):
                first = HALF * half + col
                result = by_vector([P, width], F32, f"result{n}{half}{col}")
                picked = g_rows[n][:].indirect(offsets(idx, first, width))
                nc.vector.tensor_tensor(result[:], picked, gated[n, half][:, col : col + width], ALU.add)
                nc.sync.dma_start(out[P * n : P * (n + 1), first : first + width], result[:])

        c_words = gathered_whole(code_words, idx2, U32, "c_words")
        c_sc = gathered_whole(code_scales, idx2, U8, "c_sc")
        for u in range(2):
            group_wa(0, 0, u, by_scalar([P, 2 * PASS], BF16, f"wa_grouped00{u}")[:], nc.scalar.copy)
        order_wb()
        for half in range(2):
            code_passes(0, half)
        for u in range(2):
            quantise_wa(0, 0, u)
        v_words[0, 0], v_words[0, 1] = gathered_whole(tok_words[0], idx, U32, "v_words0")
        for half in range(2):
            gather_token_scales(half)
            token_passes(0, half, 0)
        for u in range(2):
            group_wa(0, 1, u, by_scalar([P, 2 * PASS], BF16, f"wa_grouped01{u}")[:], nc.scalar.copy)
        quantise_wa(0, 1, 0)
        gather_tokens(1, 0)
        quantise_wa(0, 1, 1)
        token_passes(0, 0, 1)
        gather_tokens(1, 1)
        token_passes(0, 1, 1)

        empty_hidden(0, 0)
        wa_grouped10 = by_vector([P, 4 * PASS], BF16, "wa_grouped10")
        for u in range(2):
            group_wa(1, 0, u, half_of(wa_grouped10, u), nc.vector.tensor_copy)
        for u in range(2):
            quantise_wa(1, 0, u)
        code_passes(1, 0)
        token_passes(1, 0, 0)
        empty_hidden(0, 1)
        h_grouped[0, 0] = by_vector([P, 4 * HALF], BF16, "h_grouped00")
        group_h(0, 0, 0, nc.vector.tensor_copy)
        h_grouped[0, 1] = by_vector([P, 4 * HALF], BF16, "wa11_then_h01")
        for u in range(2):
            group_wa(1, 1, u, half_of(h_grouped[0, 1], u), nc.vector.tensor_copy)
        for u in range(2):
            quantise_wa(1, 1, u)
        token_passes(1, 0, 1)
        token_passes(1, 1, 1)
        code_passes(1, 1)
        token_passes(1, 1, 0)

        group_h(0, 0, 1, nc.scalar.copy)
        for u in range(2):
            group_h_on_gpsimd(0, 1, u)
        empty_hidden(1, 0)
        gather_residual(0)
        h_grouped[1, 0] = h_grouped[1, 1] = by_vector([P, 4 * HALF], BF16, "h10_then_h11")
        for u in range(2):
            group_h(1, 0, u, nc.vector.tensor_copy)
        for g in range(2):
            group_w1(0, g)
        for g in range(2):
            quantise_h(g, 0)
        empty_hidden(1, 1)
        quantise_w1(0)
        quantise_h(0, 1)
        group_h_on_gpsimd(1, 1, 0)
        group_h(1, 1, 1, nc.scalar.copy)

        for n in range(2):
            gate_passes(n, 0)
        for n in range(2):
            value_passes(n, 0)
        gather_residual(1)
        quantise_h(1, 1)
        for n in range(2):
            gate_value(n, 0)
        finished = [h_grouped[1, 1], resid[0], resid[1]]
        for n in range(2):
            add_residual(n, 0, finished[n])
        for g in range(2):
            group_w1(1, g)
        for n in range(2):
            products(n, 1)
        gather_residual(2)
        quantise_w1(1)
        for n in range(2):
            gate_value(n, 1)
            add_residual(n, 1, finished[n])
            store_rows(n, finished[n])

        for n in (2, 3):
            for half in range(2):
                gate_passes(n, half)
            for half in range(2):
                value_passes(n, half)
        for half in range(2):
            gate_value(2, half)
            add_residual(2, half, finished[2])
        store_rows(2, finished[2])
        for g in range(2):
            group_w1(2, g)
        gather_residual(3)
        for half in range(2):
            gate_value(3, half)

        for n in (4, 5):
            for half in range(2):
                gate_passes(n, half)
        quantise_w1(2)
        for half in range(2):
            add_residual(3, half, w1_grouped[2])
        store_rows(3, w1_grouped[2])
        resid_40 = gathered(g_rows[4], idx, 0, F32, "resid40")
        for n in (4, 5):
            for half in range(2):
                value_passes(n, half)
                gate_value(n, half)
        nc.gpsimd.tensor_tensor(gated[4, 0][:], gated[4, 0][:], resid_40, ALU.add)
        nc.sync.dma_start(out[P * 4 : P * 5, :HALF], gated[4, 0][:])
        gather_add_store(4, 1, 1)
        gather_add_store(5, 0, 1)
        gather_add_store(5, 1, 2)
